import numpy as np, ml_dtypes
CORES = [1,5,17,21,33,37,49,53]
N = 8
BF = ml_dtypes.bfloat16
T, NC, GY, W, H, HW = 512, 4096, 64, 128, 32, 4096
LZ, ZS, UN, P = 4096, 3, 16, 2
def poses(rng, a, b):
    p = np.zeros((N, 8, 6), np.int64); p[..., 0] = a; p[..., 1] = b
    p[..., 2] = rng.integers(-4000, 4001, (N, 8)) - (256 * a + 4 * GY * b)
    p[..., 3] = rng.integers(-4000, 4001, (N, 8)) + 16384 - (4 * GY * a - 256 * b)
    p[..., 4] = rng.integers(-5 * H, 5 * H + 1, (N, 8)); p[..., 5] = rng.integers(LZ // 16, LZ // 3, (N, 8))
    return p.astype(np.int32)
def image(v):
    return v.astype(np.float32).astype(BF)
def setup_inputs(rng):
    w = rng.random((N, 1)) * 2 * np.pi; j = rng.integers(-2, 3, (2, N, 8))
    a = np.clip(np.rint(64 * np.cos(w)).astype(np.int64) + j[0], -64, 64); b = np.clip(np.rint(64 * np.sin(w)).astype(np.int64) + j[1], -64, 64)
    v = rng.integers(-31, 32, (N, 16, HW)); v[:, :2] = rng.integers(-12, 13, (N, 2, HW)); v[:, 15] = rng.integers(0, 256, (N, HW))
    return {"cam": image(v), "lens": rng.integers(0, 1024, (N, 8, LZ)).astype(np.int32), "pose": poses(rng, a, b)}
def setup_inputs_ends(rng):
    d = setup_inputs(rng); p = d["pose"]; e = d["lens"]; top = 32768 - 512 * (GY - 1)
    p[..., 0] = 64; p[..., 1] = 0; p[..., 2] = rng.integers(-2000, 2001, (N, 8)) - 16384; p[..., 5] = LZ
    p[..., 3] = rng.permuted(np.tile(np.array([0, -1, top - 1, top]), (N, 2, 1)), axis=2).reshape(N, 8)
    e[:] = np.where(rng.random(e.shape) < 0.75, e, rng.choice(np.array([0, 1, 4095]), e.shape))
    e[:, :, 0] = rng.integers(1, 256, (N, 8)); e[:, :, LZ - 1] = rng.integers(1, 256, (N, 8)); e[:, 4:] = 1024
    p[:, 4, 4] = -2 * H - 1; p[:, 5, 4] = 2 * H; p[:, 6, 4] = 2 * H - 1; p[:, 7, 4] = -2 * H
    p[:, 6, 2] = 384 - 16384; p[:, 7, 2] = -16384
    return d
def setup_inputs_ties(rng):
    d = setup_inputs(rng); a = 16 * rng.integers(1, 4, (N, 8)) * rng.choice(np.array([-1, 1]), (N, 8)); b = 16 * rng.integers(-2, 3, (N, 8))
    p = poses(rng, a, b); p[..., 3] = p[..., 3] & -128
    p[..., 5] = rng.permuted(np.tile(UN * np.array([0, 1, 32, 64]), (N, 2, 1)), axis=2).reshape(N, 8)
    d["pose"] = p; return d
def setup_inputs_one(rng):
    d = setup_inputs(rng); d["lens"][:, :4] = 0; d["pose"][:, :2, 5] = LZ
    v = d["cam"].astype(np.float32); v[:, :2] = rng.choice(np.array([-31, 31]), (N, 2, HW)); d["cam"] = image(v); return d
def setup_inputs_blind(rng):
    d = setup_inputs(rng); q = rng.permutation(N); p = d["pose"]
    p[q[0], :, 0] = 64; p[q[0], :, 1] = 0; p[q[0], :, 3] = -49152; p[q[1], :, 5] = 0
    v = d["cam"].astype(np.float32); v[q[2], 15] = 0; d["cam"] = image(v); return d
def setup_inputs_spread(rng):
    d = setup_inputs(rng); p = d["pose"]
    v = rng.integers(-31, 32, (N, 16, HW)); v = np.sign(v) * (np.abs(v) >> rng.integers(0, 6, (N, 1, HW))); v[:, 15] = rng.integers(0, 256, (N, HW)) >> rng.integers(0, 3, (N, HW))
    d["cam"] = image(v); d["lens"] = (rng.integers(0, 4096, (N, 8, LZ)) >> rng.integers(0, 8, (N, 8, LZ))).astype(np.int32)
    y = rng.integers(-4095, 4096, (N, 8)); p[..., 4] = np.sign(y) * (np.abs(y) >> rng.integers(0, 8, (N, 8)))
    p[..., 5] = rng.integers(LZ // 4, LZ + 1, (N, 8)) >> rng.integers(0, 6, (N, 8)); return d
def check_inputs(d):
    bad = []; c = d["cam"].astype(np.float32); p = d["pose"].astype(np.int64); e = d["lens"]
    if not (np.isfinite(c).all() and (c == np.floor(c)).all()): bad.append("whole numbers in cam")
    if not (np.abs(c[:, :15]) <= 31).all(): bad.append("features")
    if not ((c[:, 15] >= 0) & (c[:, 15] <= 255)).all(): bad.append("depth")
    if not ((e >= 0) & (e <= 4095)).all(): bad.append("lens")
    if not (np.abs(p[..., 0:2]) <= 64).all(): bad.append("turning numbers")
    if not (np.abs(p[..., 2:4]) <= 49152).all(): bad.append("offsets")
    if not (np.abs(p[..., 4]) <= 4095).all(): bad.append("height")
    if not ((p[..., 5] >= 0) & (p[..., 5] <= LZ)).all(): bad.append("tolerance")
    return bad
def reference(cam, lens, pose):
    c = np.arange(NC); sx = np.zeros(NC, np.int64); sy = np.zeros(NC, np.int64)
    im = np.concatenate([cam.astype(np.float32), np.zeros((N, 16, 1), np.float32)], 2).astype(np.int64)
    for k in range(P):
        gx = 8 * (c & 63) + sx; gy = 8 * (c >> 6) + sy; s = np.zeros((16, NC), np.int64)
        for r in range(N):
            for g in range(8):
                a, b, tx, tz, h, tol = [int(v) for v in pose[r, g]]
                x = (a * gx + b * gy + tx) >> 5; z = (a * gy - b * gx + tz) >> ZS
                near = (z >= 0) & (z < LZ); m = lens[r, g][np.where(near, z, 0)].astype(np.int64)
                u = ((x * m) >> 12) + W // 2; v = ((h * m) >> 12) + H // 2
                seen = near & (u >= 0) & (u < W) & (v >= 0) & (v < H)
                t = im[r][:, np.where(seen, W * v + u, HW)]
                s += t * (np.abs(UN * t[15] - z) <= tol)
        sx = np.minimum(np.maximum(s[0], -31), 31); sy = np.minimum(np.maximum(s[1], -31), 31)
    y = np.ascontiguousarray(s.reshape(16, N, T).transpose(1, 0, 2)).astype(np.float32)
    return {"y": y}

@@ -1,0 +1,547 @@
+from concourse.bass import DstId, RemoteDMATransfer
+from concourse.mybir import AluOpType as ALU, ActivationFunctionType as AF
+
+N = 8
+F32, BF, I32, U16, F16 = "float32", "bfloat16", "int32", "uint16", "float16"
+MAGIC = 12582912.0
+WL, WC = 4128, 4112
+
+SCRATCH = {
+    "lensi": ("sbuf", [128, 256], I32), "posei": ("sbuf", [8, 8], I32), "posef": ("sbuf", [8, 8], F32),
+    "hi": ("sbuf", [128, 256], BF), "lo": ("sbuf", [128, 256], BF), "vt": ("sbuf", [128, 256], BF),
+    "vi": ("sbuf", [128, 256], I32), "va": ("sbuf", [128, 256], I32),
+    "winl": ("sbuf", [128, WL], BF), "winc": ("sbuf", [128, WC], BF),
+    "ones": ("sbuf", [128, 128], F32), "rep": ("sbuf", [8, 128], F32), "id32": ("sbuf", [128, 128], F32),
+    "ones2": ("sbuf", [128, 256], F32), "pm": ("sbuf", [128, 256], F32), "kb": ("sbuf", [128, 128], F32),
+    "rst": ("sbuf", [128, 128], F32),
+    "idbf": ("sbuf", [128, 128], BF), "id16": ("sbuf", [128, 128], F16),
+    "d16": ("sbuf", [128, 16], I32), "d16a": ("sbuf", [128, 16], I32),
+    "e16i": ("sbuf", [32, 256], I32), "e16a": ("sbuf", [32, 256], I32), "e16": ("sbuf", [32, 256], F32),
+    "sell": ("sbuf", [128, 16], BF), "seld": ("sbuf", [128, 16], BF), "selc": ("sbuf", [128, 16], BF),
+    "selt": ("sbuf", [128, 8], F32),
+    "col": ("sbuf", [128, 16], F32), "ct": ("sbuf", [128, 200], F32), "pt": ("sbuf", [128, 256], F32),
+    "kk": ("sbuf", [128, 256], F32), "selw": ("sbuf", [128, 32], F32), "s96": ("sbuf", [128, 128], F32),
+    "ww": ("sbuf", [32, 256], BF), "tolt": ("sbuf", [128, 128], F32),
+    "bndc": ("sbuf", [32, 8], F32), "bnd": ("sbuf", [32, 8], F32),
+    "frecv": ("sbuf", [128, N, 64], F16), "fout": ("sbuf", [128, N, 64], F16), "yb": ("sbuf", [64, 128], F32),
+}
+for _h in range(2):
+    SCRATCH["mk%d" % _h] = ("sbuf", [128, 128], F32)
+    SCRATCH["mv%d" % _h] = ("sbuf", [128, 128], F32)
+    SCRATCH["sc%d" % _h] = ("sbuf", [128, 128], F32)
+    SCRATCH["snd%d" % _h] = ("sbuf", [128, 32], BF)
+    SCRATCH["rcv%d" % _h] = ("sbuf", [128, N, 32], BF)
+    SCRATCH["sh%d" % _h] = ("sbuf", [32, 128], BF)
+    SCRATCH["fo%d" % _h] = ("sbuf", [128, 128], U16)
+    SCRATCH["gf%d" % _h] = ("sbuf", [128, 2048], BF)
+    for _p in (1, 2):
+        for _n, _d in (("zo", U16), ("po", U16), ("xi", I32), ("ui", I32), ("nz", F32), ("w", F32), ("q", F32), ("s", F32), ("pen", BF)):
+            SCRATCH["%s%d%d" % (_n, _p, _h)] = ("sbuf", [128, 128], _d)
+        SCRATCH["gl%d%d" % (_p, _h)] = ("sbuf", [128, 2048], BF)
+        SCRATCH["gd%d%d" % (_p, _h)] = ("sbuf", [128, 2048], BF)
+    for _b in "abc":
+        SCRATCH["p%s%d" % (_b, _h)] = ("psum", [128, 512], F32)
+SCRATCH["p6"] = ("psum", [128, 512], F32)
+SCRATCH["p7"] = ("psum", [128, 512], F32)
+
+SEMAPHORES = ["pe", "dve", "act", "pool", "dl", "dp", "dw", "dc", "dy", "xa0", "xa1", "fa", "fb", "ls"]
+
+CUT = {"early": 3, "plain": 64, "b": (22, 6, 6, 22), "c1": (26, 4, 16), "c1a": 22, "x": (48, 10), "c2": (28, 24, 6), "c2a": 22,
+       "f": 14, "late": 5}
+
+
+def _count(mask):
+    return bin(mask).count("1")
+
+
+def _masks(topo, cores, src):
+    off = [topo.mask(src, c) for c in cores if topo.chip(c) != topo.chip(src)]
+    on = [topo.mask(src, c) for c in cores if c != src and topo.chip(c) == topo.chip(src)]
+    moff = off[0]
+    for m in off:
+        moff &= m
+    mon = on[0] & ~moff
+    return moff, mon
+
+
+def _blocks(topo, cores, perm, rank):
+    seq, homes = [], []
+    for h in range(2):
+        home = [t for t in range(4) if topo.chip(cores[perm[4 * h + t]]) == topo.chip(cores[rank])][0]
+        seq += [4 * h + (home + d) % 4 for d in (1, 2, 3)]
+        homes.append(4 * h + home)
+    mine = perm.index(rank)
+    return seq + [b for b in homes if b != mine] + [mine]
+
+
+def _emit(g, T, ops):
+    queue = {"pe": g.tensor, "dve": g.vector, "act": g.scalar, "pool": g, "sync": g.sync}
+    counted = ("pe", "dve", "act", "pool")
+    last_w, readers, bank = {}, {}, {}
+    known = {e: {} for e in queue}
+    place = {e: 0 for e in counted}
+    for o in ops:
+        deps = []
+        for r in o["r"]:
+            if r in last_w:
+                deps.append(last_w[r])
+        for w in o["w"]:
+            if w in last_w:
+                deps.append(last_w[w])
+            deps.extend(readers.get(w, []))
+        for b in o["b"]:
+            if b in bank and bank[b]["e"] != o["e"]:
+                deps.append(bank[b])
+        if o["tok"] is None and o["e"] in counted:
+            place[o["e"]] += 1
+            o["key"] = (o["e"], place[o["e"]])
+        else:
+            o["key"] = o["tok"]
+        o["waits"] = []
+        if o["e"] in queue:
+            k = known[o["e"]]
+            for d in sorted(deps, key=lambda d: -d["n"]):
+                s, v = d["key"]
+                if k.get(s, 0) < v:
+                    o["waits"].append(d)
+                    d["used"] = True
+                    k[s] = v
+                    for s2, v2 in d["seen"].items():
+                        if k.get(s2, 0) < v2:
+                            k[s2] = v2
+            o["seen"] = dict(k)
+        else:
+            o["seen"] = {}
+        for r in o["r"]:
+            readers.setdefault(r, []).append(o)
+        for w in o["w"]:
+            last_w[w] = o
+            readers[w] = []
+        for b in o["b"]:
+            bank[b] = o
+    total = {e: 0 for e in counted}
+    for o in ops:
+        if o["tok"] is None and o["used"]:
+            total[o["e"]] += 1
+            o["val"] = total[o["e"]]
+        elif o["tok"] is not None:
+            o["val"] = o["tok"][1]
+    for o in ops:
+        if o["e"] not in queue:
+            continue
+        for d in o["waits"]:
+            queue[o["e"]].wait_ge(T.sem[d["key"][0]], d["val"])
+        ins = o["f"]()
+        if o["tok"] is None and o["used"]:
+            ins.then_inc(T.sem[o["e"]], 1)
+        elif o["dma"]:
+            ins.then_inc(T.sem[o["tok"][0]], 16)
+
+
+def rank_program(g, core, T, topo):
+    rank = T.rank_of(core)
+    if rank is None:
+        return
+    cores = list(T.cores)
+    by_chip = {}
+    for r, c in enumerate(cores):
+        by_chip.setdefault(topo.chip(c), []).append(r)
+    perm = [rs[0] for rs in by_chip.values()] + [rs[1] for rs in by_chip.values()]
+    moff, mon = _masks(topo, cores, core)
+    others = [r for r in range(N) if r != rank]
+    near = [r for r in others if topo.chip(cores[r]) == topo.chip(core)]
+    far = [r for r in others if r not in near]
+    incs = {}
+    for r in others:
+        a, b = _masks(topo, cores, cores[r])
+        incs[r] = _count(b if r in near else a)
+    arrive = sum(incs.values())
+    is_late = lambda src, dst: _blocks(topo, cores, perm, src).index(perm.index(dst)) >= CUT["late"]
+    late = [r for r in others if is_late(r, rank)]
+    early = [r for r in others if r not in late]
+
+    V, A, PE, S = g.vector, g.scalar, g.tensor, g.sync
+    ops = []
+
+    def op(e, f, r=(), w=(), b=(), tok=None, dma=False):
+        w = list(w)
+        if e == "pool" and tok is None:
+            w.append("q7")
+        ops.append({"e": e, "f": f, "r": list(r), "w": w, "b": list(b), "tok": tok, "dma": dma,
+                    "used": False, "n": len(ops)})
+
+    def ts(out, in0, s1, s2, o0, o1=None):
+        if o1 is None:
+            return lambda: V.tensor_scalar(out, in0, s1, None, o0)
+        return lambda: V.tensor_scalar(out, in0, s1, s2, o0, o1)
+
+    def tt(out, a, b, o):
+        return lambda: V.tensor_tensor(out, a, b, o)
+
+    def act(out, in_, func, bias=0.0, scale=1.0):
+        return lambda: A.activation(out, in_, func, bias=bias, scale=scale)
+
+    def mms(lst):
+        def f():
+            ins = None
+            for (out, lhsT, rhs, st, sp) in lst:
+                ins = PE.matmul(out, lhsT, rhs, st, sp)
+            return ins
+        return f
+
+    def iota(out, pattern, base, cm, flt):
+        if flt:
+            return lambda: g.iota(out, pattern, base, cm, allow_small_or_imprecise_dtypes=True)
+        return lambda: g.iota(out, pattern, base, cm)
+
+    col = lambda j: T.col[:, j:j + 1]
+    ICOL, HCOL, T1, T2 = 0, 4, 8, 12
+    CX, CZ = 0, 100
+    ktol = T.ct[:, CZ + 96:CZ + 97]
+
+    def cam_load(q):
+        op("sync", lambda: S.dma_start(T.winc[16 * q:16 * q + 16, 0:4096], T.cam[:]), w=["winc%d" % q], tok=("dc", 128), dma=True)
+
+    op("sync", lambda: S.dma_start(T.lensi[:], T.lens[:]), w=["lensi"], tok=("dl", 16), dma=True)
+    op("act", lambda: A.dma_start(T.posei[0:8, 0:6], T.pose[:]), w=["posei"], tok=("dp", 16), dma=True)
+    for q in range(CUT["early"]):
+        cam_load(q)
+    op("dve", lambda: V.memset(T.winl[:, 0:1024], 8192.0), w=["wl0"])
+    op("dve", lambda: V.memset(T.kk[:, :], 0.0), w=["kk", "kk0", "kk32", "kk64"])
+    op("dve", lambda: V.memset(T.ct[:, :], 0.0), w=["ct", "cta", "ctb", "ctc", "ctd", "cte", "ktol"])
+    op("act", act(T.winl[:, 3104:WL], T.winl[:, 0:1024], AF.Copy), r=["wl0"], w=["wl2"])
+    op("dve", lambda: V.memset(T.winl[:, 1024:3104], 8192.0), w=["wl1"])
+    op("pool", iota(T.d16[:, :], [[-1, 16]], 0, 1, False), w=["d16"])
+    op("pool", iota(T.ones[:, :], [[0, 128]], 1, 0, True), w=["ones"])
+    op("pool", lambda: g.affine_select(T.rep[0:8, :], T.ones[0:8, :], [[1, 8], [0, 16]], ALU.is_equal, 0.0, 0, -1), r=["ones"], w=["rep"])
+    op("pool", lambda: g.affine_select(T.id32[:, :], T.ones[:, :], [[-1, 128]], ALU.is_equal, 0.0, 0, 1), r=["ones"], w=["id32"])
+    op("pool", iota(T.kk[0:1, :], [[0, 64], [16, 4]], 0, 0, True), w=["kk0"])
+    for h in range(2):
+        own = perm[4 * h:4 * h + 4]
+        if all(own[t + 1] - own[t] == own[1] - own[0] for t in range(3)):
+            op("pool", iota(T.kk[32:33, 128 * h:128 * h + 128], [[8 * (own[1] - own[0]), 4], [1, 8], [0, 4]], 8 * own[0], 0, True),
+               r=["kk32"], w=["kk32_%d" % h])
+        else:
+            for t in range(4):
+                op("pool", iota(T.kk[32:33, 128 * h + 32 * t:128 * h + 32 * t + 32], [[1, 8], [0, 4]], 8 * own[t], 0, True),
+                   r=["kk32"], w=["kk32_%d" % h])
+    op("dve", ts(T.d16a[:, :], T.d16[:, :], 15, None, ALU.bitwise_and), r=["d16"], w=["d16a"])
+    op("dve", lambda: V.tensor_copy(T.posef[0:8, 0:6], T.posei[0:8, 0:6]), r=["posei"], w=["posef"])
+    op("dve", lambda: V.tensor_copy(col(ICOL), T.d16a[:, 0:1]), r=["d16a"], w=["icol"])
+    op("pe", mms([(T.p6[:, 0:6], T.rep[0:8, :], T.posef[0:8, 0:6], True, True)]), r=["rep", "posef"], b=["p6"])
+    op("dve", lambda: V.tensor_copy(T.hi[:, :], T.lensi[:, :]), r=["lensi"], w=["hi"])
+    op("act", act(col(HCOL), T.p6[:, 4:5], AF.Identity, scale=2.0 ** -12), w=["hcol"], b=["p6"])
+    op("act", act(T.ct[:, CX:CX + 33:32], T.p6[:, 0:2], AF.Copy), w=["cta"], b=["p6"])
+    op("act", act(T.ct[:, CZ:CZ + 1], T.p6[:, 1:2], AF.Identity, scale=-1.0), w=["ctb"], b=["p6"])
+    op("act", act(col(T1), T.p6[:, 2:3], AF.Identity, bias=-15.5 / 8, scale=0.125), w=["t1"], b=["p6"])
+    op("act", act(col(T2), T.p6[:, 3:4], AF.Identity, bias=16 - 3.5 / 8, scale=0.125), w=["t2"], b=["p6"])
+    op("act", act(col(T2 + 1), T.p6[:, 5:6], AF.Relu, bias=4095.0, scale=-1.0), w=["t3"], b=["p6"])
+    op("act", act(T.ct[:, CZ + 32:CZ + 33], T.p6[:, 0:1], AF.Copy), w=["ctc"], b=["p6"])
+    op("act", act(T.ct[:, CX + 64:CX + 65], col(ICOL), AF.Identity, bias=col(T1), scale=T.ct[:, CX:CX + 1]), r=["icol", "t1", "cta"], w=["ctd"])
+    op("act", act(T.ct[:, CZ + 64:CZ + 65], col(ICOL), AF.Identity, bias=col(T2), scale=T.ct[:, CZ:CZ + 1]), r=["icol", "t2", "ctb"], w=["cte"])
+    op("act", act(ktol, col(T2 + 1), AF.Identity, bias=4095.0 * 4096, scale=-4096.0), r=["t3"], w=["ktol"])
+    op("sync", lambda: S.dma_start(T.winl[0:128:16, 16:4112], T.hi[:, :]), r=["hi", "wl0", "wl1", "wl2"], w=["wlhi"], tok=("dw", 48), dma=True)
+    op("dve", ts(T.vi[:, :], T.lensi[:, :], col(HCOL), 15.5 + 2.0 ** -13, ALU.mult, ALU.add), r=["lensi", "hcol"], w=["vi"])
+    op("dve", tt(T.lo[:, 0:128], T.lensi[:, 0:128], T.hi[:, 0:128], ALU.subtract), r=["lensi", "hi"], w=["lo0"])
+    op("dve", ts(T.va[:, :], T.vi[:, :], 0x7FFFFFFF, None, ALU.bitwise_and), r=["vi"], w=["va"])
+    op("dve", tt(T.lo[:, 128:256], T.lensi[:, 128:256], T.hi[:, 128:256], ALU.subtract), r=["lensi", "hi"], w=["lo1"])
+    op("sync", lambda: S.dma_start(T.winl[1:128:16, 16:4112], T.lo[:, :]), r=["lo0", "lo1"], w=["wllo"], tok=("dw", 48), dma=True)
+    op("dve", ts(T.vt[:, :], T.va[:, :], 128.0, None, ALU.mult), r=["va"], w=["vt"])
+    op("sync", lambda: S.dma_start(T.winl[2:128:16, 16:4112], T.vt[:, :]), r=["vt"], w=["wlvt"], tok=("dw", 48), dma=True)
+    for q in range(CUT["early"], 8):
+        cam_load(q)
+    op("dve", lambda: V.memset(T.kk[64:65, :], 1.0), w=["kk64"])
+    op("dve", lambda: V.memset(T.ones2[:, :], 1.0), w=["ones2"])
+    op("pool", lambda: g.affine_select(T.pm[:, :], T.ones2[:, :], [[-1, 16], [-16, 8], [1000, 2]], ALU.is_equal, 0.0, 0, 1), r=["ones2"], w=["pm"])
+    op("pool", iota(T.e16i[:, :], [[0, 16], [-1, 16]], 0, 1, False), w=["e16i"])
+    op("pool", iota(T.bndc[:, 0:2], [[-62, 2]], 31, 0, True), w=["bndc"])
+    op("pool", lambda: g.affine_select(T.bnd[:, 0:1], T.bndc[:, 0:1], [[0, 1]], ALU.is_ge, 31.0 / 512, 15, -1), r=["bndc"], w=["bnd0"])
+    op("pool", lambda: g.affine_select(T.bnd[:, 4:5], T.bndc[:, 1:2], [[0, 1]], ALU.is_ge, -31.0 / 512, 15, -1), r=["bndc"], w=["bnd1"])
+    ctall = ["ct", "cta", "ctb", "ctc", "ctd", "cte", "ktol"]
+    op("pe", mms([(T.p7[0:97, 0:128], T.ct[:, CX:CX + 97], T.id32[:, :], True, True),
+                  (T.p7[0:97, 128:256], T.ct[:, CZ:CZ + 97], T.id32[:, :], True, True)]), r=ctall + ["id32"], b=["p7"])
+    op("act", act(T.pt[0:97, :], T.p7[0:97, 0:256], AF.Copy), w=["pt"], b=["p7"])
+    kkall = ["kk", "kk0", "kk32_0", "kk32_1", "kk64"]
+
+    def z_base(h, stop):
+        op("pe", mms([(T["pa%d" % h][:, 0:128], T.pt[0:97, 128:256], T.kk[0:97, 128 * h:128 * h + 128], True, stop)]),
+           r=kkall + ["pt"], b=["pa%d" % h])
+
+    def x_base(h, stop):
+        op("pe", mms([(T["pb%d" % h][:, 256:384], T.kk[0:97, 128 * h:128 * h + 128], T.pt[0:97, 0:128], True, stop)]),
+           r=kkall + ["pt"], b=["pb%d" % h])
+
+    def a_zo(p, h):
+        n = "%d%d" % (p, h)
+        op("dve", ts(T["zo" + n][:, :], T["pa%d" % h][:, 0:128], 15.0, 4112.0, ALU.max, ALU.min), w=["zo" + n], b=["pa%d" % h])
+
+    def a_x(p, h):
+        n = "%d%d" % (p, h)
+        op("dve", ts(T["xi" + n][:, :], T["pb%d" % h][:, 256:384], 0.25, None, ALU.mult), w=["xi" + n], b=["pb%d" % h])
+
+    def a_nz(p, h):
+        n = "%d%d" % (p, h)
+        op("act", act(T["nz" + n][:, :], T["pa%d" % h][:, 0:128], AF.Identity, bias=-MAGIC, scale=-1.0), w=["nz" + n], b=["pa%d" % h])
+
+    wl = ["wl0", "wl1", "wl2", "wlhi", "wllo", "wlvt"]
+    wc = ["winc%d" % q for q in range(8)] + ["wcz"]
+    gall = lambda out, k0=0, k1=128: ["%s_%d" % (out, k) for k in range(k0, k1, 2)]
+
+    def gather(e, out, off, k0, k1):
+        lens = out[:2] == "gl"
+        win = T.winl[:, 0:WL] if lens else T.winc[:, 0:WC]
+        src = lambda: win.indirect(T[off][:, k0:k1])
+        dst = T[out][:, 16 * k0:16 * k1]
+        if e == "dve":
+            f = lambda: V.tensor_copy(dst, src())
+        else:
+            f = lambda: A.activation(dst, src(), AF.Copy)
+        op(e, f, r=[off] + (wl if lens else wc), w=gall(out, k0, k1))
+
+    def slot(out, off, seq):
+        vtot = sum(x[1] for x in seq if isinstance(x, tuple) and x[0] == "v")
+        lo, hi = 0, 128
+        for x in seq:
+            if not isinstance(x, tuple):
+                x()
+            elif x[0] == "v":
+                gather("dve", out, off, lo, lo + x[1])
+                lo += x[1]
+            else:
+                n = hi - vtot if x[1] is None else x[1]
+                gather("act", out, off, hi - n, hi)
+                hi -= n
+        assert lo == hi
+
+    def x_lens(p, h):
+        n = "%d%d" % (p, h)
+        pb, gl = T["pb%d" % h], T["gl" + n]
+        op("pe", mms([(pb[:, i:256:16], gl[:, i:2048:16], T.sell[:, :], p == 1, p == 1 or i == 15) for i in range(16)]),
+           r=gall("gl" + n) + ["sell0", "sell1"], b=["pb%d" % h])
+
+    def ktol_start(h):
+        op("pe", mms([(T["pb%d" % h][:, 0:256], T.s96[0:97, :], T.pt[0:97, :], True, False)]), r=["s96", "pt"], b=["pb%d" % h])
+
+    def b_steps(p, h):
+        n = "%d%d" % (p, h)
+        pa, pb = T["pa%d" % h], T["pb%d" % h]
+
+        def b1():
+            op("dve", tt(T["w" + n][:, :], T["xi" + n][:, :], pb[:, 0:128], ALU.mult), r=["xi" + n], w=["w" + n], b=["pb%d" % h])
+
+        def b2():
+            op("dve", ts(T["ui" + n][:, :], T["w" + n][:, :], 2.0 ** -12, 63.5 + 2.0 ** -13, ALU.mult, ALU.add), r=["w" + n], w=["ui" + n])
+
+        def b3():
+            op("dve", tt(T["s" + n][:, :], T["ui" + n][:, :], pb[:, 128:256], ALU.add), r=["ui" + n], w=["s" + n], b=["pb%d" % h])
+            op("pe", mms([(pa[:, 128:256], T["s" + n][:, :], T.id32[:, :], True, True)]), r=["s" + n, "id32"], b=["pa%d" % h])
+
+        def b4():
+            if p == 1:
+                op("dve", ts(T["po" + n][:, :], pa[:, 128:256], 4096.0, None, ALU.min), w=["po" + n], b=["pa%d" % h])
+            else:
+                op("dve", ts(T["po" + n][:, :], pa[:, 128:256], ktol, 4096.0, ALU.subtract, ALU.min), r=["ktol"], w=["po" + n], b=["pa%d" % h])
+        c = CUT["b"]
+        return [("v", c[0]), ("a", None), b1, ("v", c[1]), b2, ("v", c[2]), b3, ("v", c[3]), b4]
+
+    def b_pen(p, h):
+        n = "%d%d" % (p, h)
+        pc, pen = T["pc%d" % h], T["pen" + n]
+        op("act", act(T["q" + n][:, :], T["w" + n][:, :], AF.Abs, bias=0.5), r=["w" + n], w=["q" + n])
+        if p == 2:
+            a_nz(p, h)
+        op("act", act(pen[:, :], T["q" + n][:, :], AF.Relu, bias=-(2.0 ** 35), scale=2.0 ** 17), r=["q" + n], w=["pen" + n])
+        if p == 1:
+            op("pe", mms([(pc[:, 2 * x:256:16], T.idbf[:, :], pen[:, 16 * x:16 * x + 16], False, False) for x in range(8)]),
+               r=["pen" + n, "idbf"], b=["pc%d" % h])
+        else:
+            op("pe", mms([(pc[:, 0:128], T["nz" + n][:, :], T.id32[:, :], True, False), (pc[:, 0:128], T.idbf[:, :], pen[:, :], False, False)]),
+               r=["pen" + n, "idbf", "id32", "nz" + n], b=["pc%d" % h])
+
+    def x_depth(p, h):
+        n = "%d%d" % (p, h)
+        pc, gd = T["pc%d" % h], T["gd" + n]
+        if p == 1:
+            lst = [(pc[:, 16 * i:16 * i + 16], gd[:, i:2048:16], T.seld[:, :], False, i == 15) for i in range(16)]
+        else:
+            lst = [(pc[:, i:128:16], gd[:, i:2048:16], T.seld[:, 0:16:2], False, i == 15) for i in range(16)]
+        op("pe", mms(lst), r=gall("gd" + n) + ["seld0", "seld1"], b=["pc%d" % h])
+
+    def c_abs(p, h):
+        pc = T["pc%d" % h]
+        op("act", act(pc[:, 256:384], pc[:, 0:256:2] if p == 1 else pc[:, 0:128], AF.Abs, bias=4096.0 * (MAGIC + 16), scale=4096.0),
+           b=["pc%d" % h])
+
+    def c_sums(h):
+        pc, sc, snd = T["pc%d" % h], T["sc%d" % h], T["snd%d" % h]
+        mk, mv = T["mk%d" % h], T["mv%d" % h]
+        return [
+            lambda: op("dve", tt(mk[:, :], pc[:, 256:384], T.tolt[:, :], ALU.is_le), r=["tolt"], w=["mk%d" % h], b=["pc%d" % h]),
+            lambda: op("dve", tt(mv[:, :], mk[:, :], pc[:, 1:256:2], ALU.mult), r=["mk%d" % h], w=["mv%d" % h], b=["pc%d" % h]),
+            lambda: op("dve", lambda: V.tensor_tensor_scan(sc[:, :], T.rst[:, :], mv[:, :], 0.0, ALU.mult, ALU.add),
+                       r=["mv%d" % h, "rst"], w=["sc%d" % h]),
+            lambda: op("dve", ts(snd[:, 0:16], sc[:, 7:128:8], MAGIC, MAGIC, ALU.add, ALU.subtract), r=["sc%d" % h], w=["sna%d" % h]),
+            lambda: op("dve", tt(snd[:, 16:32], sc[:, 7:128:8], snd[:, 0:16], ALU.subtract), r=["sc%d" % h, "sna%d" % h], w=["snb%d" % h])]
+
+    left = [0]
+
+    def dst_id(r):
+        rid, pid, _se = topo.addr(cores[r])
+        return DstId(rid=rid, pnc=pid)
+
+    def send_shift(h):
+        snd, land = T["snd%d" % h][:, :], T["rcv%d" % h][:, rank, :]
+        sem = T.sem["xa%d" % h]
+
+        def f():
+            tr = [RemoteDMATransfer(dst_ids=[dst_id(r) for r in grp], dma_engine_mask=m, remote_sem=sem,
+                                    srcs=[snd], dsts=[land for _r in grp]) for grp, m in ((far, moff), (near, mon))]
+            return g.remote_dma_fused(tr, local_sem=T.sem.ls)
+        left[0] += _count(moff) + _count(mon)
+        op("pool", f, r=["sna%d" % h, "snb%d" % h], tok=("ls", 0))
+
+    def shift_own(h):
+        op("pe", mms([(T["pc%d" % h][0:32, 384:512], T["snd%d" % h][:, :], T.idbf[:, :], True, False)]),
+           r=["sna%d" % h, "snb%d" % h, "idbf"], b=["pc%d" % h])
+
+    def shift_sum(h):
+        pa, pb, pc, sh = T["pa%d" % h], T["pb%d" % h], T["pc%d" % h], T["sh%d" % h]
+        op("ext", None, w=["rcv%d" % h], tok=("xa%d" % h, arrive))
+        op("pe", mms([(pc[0:32, 384:512], T["rcv%d" % h][:, r, :], T.idbf[:, :], False, r == others[-1]) for r in others]),
+           r=["rcv%d" % h], b=["pc%d" % h])
+        op("dve", ts(sh[:, :], pc[0:32, 384:512], T.bnd[:, 4:5], T.bnd[:, 0:1], ALU.max, ALU.min), r=["bnd0", "bnd1"], w=["sh%d" % h], b=["pc%d" % h])
+        op("pe", mms([(pa[:, 0:128], T.ww[:, 128:256], sh[:, :], False, True)]), r=["ww", "sh%d" % h], b=["pa%d" % h])
+        op("pe", mms([(pb[:, 256:384], sh[:, :], T.ww[:, 0:128], False, True)]), r=["ww", "sh%d" % h], b=["pb%d" % h])
+
+    def c_keep(h):
+        pa, pc = T["pa%d" % h], T["pc%d" % h]
+        op("dve", tt(T["mk%d" % h][:, :], T["s2%d" % h][:, :], pc[:, 256:384], ALU.max), r=["s2%d" % h], w=["mk%d" % h], b=["pc%d" % h])
+        op("pe", mms([(pa[:, 256:384], T["mk%d" % h][:, :], T.id32[:, :], True, True)]), r=["mk%d" % h, "id32"], b=["pa%d" % h])
+
+    def c_off(h):
+        op("dve", ts(T["fo%d" % h][:, :], T["pa%d" % h][:, 256:384], ktol, 4096.0, ALU.subtract, ALU.min), r=["ktol"], w=["fo%d" % h], b=["pa%d" % h])
+
+    fbank = lambda j: (("pb0", "pc0", "pb1")[j % 3], 64 * (j // 3))
+
+    def f_sum(b, j):
+        h, t = divmod(b, 4)
+        bk, c0 = fbank(j)
+        gf = T["gf%d" % h]
+        op("pe", mms([(T[bk][:, c0 + x:c0 + 64:4], gf[:, 512 * t + 128 * x:512 * t + 128 * x + 128], T.selc[:, :], True, True) for x in range(4)]),
+           r=gall("gf%d" % h, 32 * t, 32 * t + 32) + ["selc"], b=[bk])
+
+    def f_out(b, j):
+        bk, c0 = fbank(j)
+        owner = perm[b]
+        src = T.fout[:, b, :]
+        op("dve", lambda: V.tensor_copy(src, T[bk][:, c0:c0 + 64]), w=["fout%d" % b], b=[bk])
+        if owner != rank:
+            m = moff if owner in far else mon
+            rid, pid, _se = topo.addr(cores[owner])
+            left[0] += _count(m)
+            sem = T.sem["fb" if is_late(rank, owner) else "fa"]
+            op("pool", lambda: g.remote_dma(T.frecv[:, rank, :], src, sem, T.sem.ls, pid, rid, m), r=["fout%d" % b], tok=("ls", 0))
+
+    z_base(0, True)
+    z_base(1, True)
+    x_base(0, True)
+    x_base(1, True)
+    op("dve", tt(T.sell[:, 0:8], T.id32[:, 0:128:16], T.id32[:, 1:128:16], ALU.add), r=["id32"], w=["sell0"])
+    op("dve", lambda: V.tensor_copy(T.sell[:, 8:16], T.id32[:, 2:128:16]), r=["id32"], w=["sell1"])
+    op("dve", lambda: V.memset(T.winc[:, 4096:WC], 0.0), w=["wcz"])
+    op("dve", lambda: V.memset(T.rst[:, :], 1.0), w=["rst"])
+    op("act", act(T.selt[:, :], T.id32[:, 1:128:16], AF.Identity, scale=2.0 ** -9), r=["id32"], w=["selt"])
+    op("act", act(T.idbf[:, :], T.id32[:, :], AF.Copy), r=["id32"], w=["idbf"])
+    op("act", act(T.seld[:, 0:16:2], T.id32[:, 15:128:16], AF.Identity, scale=16.0), r=["id32"], w=["seld0"])
+    op("act", act(T.kb[:, :], T.ones[:, :], AF.Identity, scale=ktol), r=["ones", "ktol"], w=["kb"])
+    op("dve", tt(T.seld[:, 1:16:2], T.id32[:, 0:128:16], T.selt[:, :], ALU.add), r=["id32", "selt"], w=["seld1"])
+    op("dve", lambda: V.memset(T.rst[:, 0:128:8], 0.0), w=["rst"])
+    a_zo(1, 0)
+    a_zo(1, 1)
+    a_nz(1, 0)
+    a_nz(1, 1)
+    a_x(1, 0)
+    a_x(1, 1)
+    op("pe", mms([(T.p6[:, 128:256], T.kb[:, :], T.pm[:, 0:256:2], True, True)]), r=["kb", "pm"], b=["p6"])
+    for h in range(2):
+        op("pe", mms([(T["pc%d" % h][:, 0:256], T["nz1%d" % h][:, :], T.pm[:, :], True, False)]), r=["nz1%d" % h, "pm"], b=["pc%d" % h])
+
+    slot("gl10", "zo10", [("v", CUT["plain"]), ("a", None)])
+    op("act", act(T.tolt[:, :], T.p6[:, 128:256], AF.Copy), w=["tolt"], b=["p6"])
+    x_lens(1, 0)
+    slot("gl11", "zo11", b_steps(1, 0))
+    x_lens(1, 1)
+    b_pen(1, 0)
+    slot("gd10", "po10", b_steps(1, 1))
+    x_depth(1, 0)
+    c = CUT["c1"]
+    seq = [("v", c[0]), ("a", CUT["c1a"]), lambda: c_abs(1, 0), lambda: b_pen(1, 1), ("a", None)]
+    steps = c_sums(0)
+    for st in steps[:-1]:
+        seq += [st, ("v", c[1])] if c[1] else [st]
+    slot("gd11", "po11", seq + [steps[-1], lambda: send_shift(0), ("v", c[2])])
+    x_depth(1, 1)
+    c_abs(1, 1)
+    fill = [lambda: op("dve", lambda: V.memset(T.selw[:, :], 0.0), w=["selw"]),
+            lambda: op("dve", lambda: V.memset(T.s96[:, :], 0.0), w=["s96"]),
+            lambda: op("dve", lambda: V.memset(T.selw[0:1, 0:16], 0.125), r=["selw"], w=["selw0"]),
+            lambda: op("dve", lambda: V.memset(T.selw[32:33, 16:32], 64.0), r=["selw"], w=["selw1"])]
+    for i, st in enumerate(c_sums(1)):
+        st()
+        if i < len(fill):
+            fill[i]()
+    send_shift(1)
+    op("dve", ts(T.e16a[:, :], T.e16i[:, :], 15, None, ALU.bitwise_and), r=["e16i"], w=["e16a"])
+    op("dve", lambda: V.memset(T.s96[96:97, :], 1.0), w=["s96"])
+    op("dve", ts(T.e16[:, :], T.e16a[:, :], 0.0, None, ALU.is_equal), r=["e16a"], w=["e16"])
+    op("pe", mms([(T.p7[0:32, 256:512], T.selw[0:97, :], T.pt[0:97, :], True, True)]), r=["selw", "selw0", "selw1", "pt"], b=["p7"])
+    for h in range(2):
+        z_base(h, False)
+        x_base(h, False)
+        shift_own(h)
+    op("dve", ts(T.selc[:, :], T.d16a[:, :], 0.0, None, ALU.is_equal), r=["d16a"], w=["selc"])
+    op("dve", tt(T.ww[:, :], T.e16[:, :], T.p7[0:32, 256:512], ALU.mult), r=["e16"], w=["ww"], b=["p7"])
+    op("dve", lambda: V.tensor_copy(T.id16[:, :], T.id32[:, :]), r=["id32"], w=["id16"])
+
+    shift_sum(0)
+    a_zo(2, 0)
+    c = CUT["x"]
+    slot("gl20", "zo20", [("a", None), lambda: a_x(2, 0), lambda: ktol_start(0), ("v", c[0]), lambda: shift_sum(1), ("v", c[1]),
+                          lambda: a_zo(2, 1), lambda: a_x(2, 1)])
+    x_lens(2, 0)
+    ktol_start(1)
+    slot("gl21", "zo21", b_steps(2, 0))
+    x_lens(2, 1)
+    b_pen(2, 0)
+    slot("gd20", "po20", b_steps(2, 1))
+    x_depth(2, 0)
+    c = CUT["c2"]
+    slot("gd21", "po21", [("v", c[0]), ("a", CUT["c2a"]), lambda: c_abs(2, 0), lambda: b_pen(2, 1), ("a", None), lambda: c_keep(0),
+                          ("v", c[1]), lambda: c_off(0), ("v", c[2])])
+    x_depth(2, 1)
+    seq = _blocks(topo, cores, perm, rank)
+    for j, b in enumerate(seq):
+        h, t = divmod(b, 4)
+        gf, fo, k0 = "gf%d" % h, "fo%d" % h, 32 * t
+        gather("act", gf, fo, k0 + CUT["f"], k0 + 32)
+        gather("dve", gf, fo, k0, k0 + CUT["f"])
+        if j == 0:
+            c_abs(2, 1)
+            c_keep(1)
+        f_sum(b, j)
+        if j > 0:
+            f_out(seq[j - 1], j - 1)
+        if j == 1:
+            c_off(1)
+    f_out(seq[7], 7)
+    op("pe", mms([(T.p6[0:64, 256:384], T.fout[:, seq[7], :], T.id16[:, :], True, False)]), r=["fout%d" % seq[7], "id16"], b=["p6"])
+    groups = [(s, grp) for s, grp in (("fa", early), ("fb", late)) if grp]
+    for s, grp in groups:
+        op("ext", None, w=[s], tok=(s, sum(incs[r] for r in grp)))
+        op("pe", mms([(T.p6[0:64, 256:384], T.frecv[:, r, :], T.id16[:, :], False, s == groups[-1][0] and r == grp[-1]) for r in grp]),
+           r=[s], b=["p6"])
+    op("dve", lambda: V.tensor_copy(T.yb[:, :], T.p6[0:64, 256:384]), w=["yb"], b=["p6"])
+    op("sync", lambda: S.dma_start(T.y[:], T.yb[:, :]), r=["yb"], tok=("dy", 16), dma=True)
+    _emit(g, T, ops)
+    g.wait_ge(T.sem.ls, left[0])
+    S.wait_ge(T.sem.dy, 16)

@@ -18,24 +18,23 @@ SCRATCH = {
     "d16": ("sbuf", [128, 16], I32), "d16a": ("sbuf", [128, 16], I32),
     "e16i": ("sbuf", [32, 256], I32), "e16a": ("sbuf", [32, 256], I32), "e16": ("sbuf", [32, 256], F32),
     "sell": ("sbuf", [128, 16], BF), "seld": ("sbuf", [128, 16], BF), "selc": ("sbuf", [128, 16], BF),
-    "selt": ("sbuf", [128, 8], F32),
-    "col": ("sbuf", [128, 16], F32), "ct": ("sbuf", [128, 200], F32), "pt": ("sbuf", [128, 256], F32),
-    "kk": ("sbuf", [128, 256], F32), "selw": ("sbuf", [128, 32], F32), "s96": ("sbuf", [128, 128], F32),
+    "selt": ("sbuf", [128, 16], F32),
+    "col": ("sbuf", [128, 24], F32), "ct": ("sbuf", [128, 144], F32), "pt": ("sbuf", [128, 256], F32),
+    "kk": ("sbuf", [128, 256], F32), "selw": ("sbuf", [128, 32], F32),
     "ww": ("sbuf", [32, 256], BF), "tolt": ("sbuf", [128, 128], F32),
     "bndc": ("sbuf", [32, 8], F32), "bnd": ("sbuf", [32, 8], F32),
     "frecv": ("sbuf", [128, N, 64], F16), "fout": ("sbuf", [128, N, 64], F16), "yb": ("sbuf", [64, 128], F32),
 }
 for _h in range(2):
-    SCRATCH["mk%d" % _h] = ("sbuf", [128, 128], F32)
-    SCRATCH["mv%d" % _h] = ("sbuf", [128, 128], F32)
-    SCRATCH["sc%d" % _h] = ("sbuf", [128, 128], F32)
+    for _n in ("mk", "mv", "sc", "sn", "ab", "kp"):
+        SCRATCH["%s%d" % (_n, _h)] = ("sbuf", [128, 128], F32)
     SCRATCH["snd%d" % _h] = ("sbuf", [128, 32], BF)
     SCRATCH["rcv%d" % _h] = ("sbuf", [128, N, 32], BF)
     SCRATCH["sh%d" % _h] = ("sbuf", [32, 128], BF)
     SCRATCH["fo%d" % _h] = ("sbuf", [128, 128], U16)
     SCRATCH["gf%d" % _h] = ("sbuf", [128, 2048], BF)
     for _p in (1, 2):
-        for _n, _d in (("zo", U16), ("po", U16), ("xi", I32), ("ui", I32), ("nz", F32), ("w", F32), ("q", F32), ("s", F32), ("pen", BF)):
+        for _n, _d in (("zo", U16), ("po", U16), ("xi", I32), ("ub", BF), ("vb", BF), ("nz", F32), ("w", F32), ("q", F32), ("pen", BF)):
             SCRATCH["%s%d%d" % (_n, _p, _h)] = ("sbuf", [128, 128], _d)
         SCRATCH["gl%d%d" % (_p, _h)] = ("sbuf", [128, 2048], BF)
         SCRATCH["gd%d%d" % (_p, _h)] = ("sbuf", [128, 2048], BF)
@@ -46,22 +45,17 @@ SCRATCH["p7"] = ("psum", [128, 512], F32)
 
 SEMAPHORES = ["pe", "dve", "act", "pool", "dl", "dp", "dw", "dc", "dy", "xa0", "xa1", "fa", "fb", "ls"]
 
-CUT = {"early": 3, "plain": 64, "b": (22, 6, 6, 22), "c1": (26, 4, 16), "c1a": 22, "x": (48, 10), "c2": (28, 24, 6), "c2a": 22,
-       "f": 14, "late": 5}
-
-
-def _count(mask):
-    return bin(mask).count("1")
+CUT = {"early": 3, "plain": 62, "b": (30, 6, 18, 10), "ba": 40, "c1": (30, 4, 12), "c1a": 20, "x": (48, 10), "c2": (48, 6, 8), "c2a": 24,
+       "f": (14, 22, 12, 14, 14, 14, 14, 14), "late": 5}
+HOME = (4, 4, 4)
 
 
 def _masks(topo, cores, src):
-    off = [topo.mask(src, c) for c in cores if topo.chip(c) != topo.chip(src)]
-    on = [topo.mask(src, c) for c in cores if c != src and topo.chip(c) == topo.chip(src)]
-    moff = off[0]
-    for m in off:
-        moff &= m
-    mon = on[0] & ~moff
-    return moff, mon
+    off = [set(topo.engines(src, c)) for c in cores if topo.chip(c) != topo.chip(src)]
+    on = [topo.engines(src, c) for c in cores if c != src and topo.chip(c) == topo.chip(src)]
+    far = sorted(set.intersection(*off))
+    rest = [e for e in on[0] if e not in far]
+    return sum(1 << e for e in far), len(far), rest[0::2] + rest[1::2]
 
 
 def _blocks(topo, cores, perm, rank):
@@ -147,15 +141,12 @@ def rank_program(g, core, T, topo):
     for r, c in enumerate(cores):
         by_chip.setdefault(topo.chip(c), []).append(r)
     perm = [rs[0] for rs in by_chip.values()] + [rs[1] for rs in by_chip.values()]
-    moff, mon = _masks(topo, cores, core)
+    moff, noff, rest = _masks(topo, cores, core)
+    mon = [sum(1 << e for e in rest[:n]) for n in HOME]
     others = [r for r in range(N) if r != rank]
     near = [r for r in others if topo.chip(cores[r]) == topo.chip(core)]
     far = [r for r in others if r not in near]
-    incs = {}
-    for r in others:
-        a, b = _masks(topo, cores, cores[r])
-        incs[r] = _count(b if r in near else a)
-    arrive = sum(incs.values())
+    incs = lambda r, step: HOME[step] if r in near else _masks(topo, cores, cores[r])[1]
     is_late = lambda src, dst: _blocks(topo, cores, perm, src).index(perm.index(dst)) >= CUT["late"]
     late = [r for r in others if is_late(r, rank)]
     early = [r for r in others if r not in late]
@@ -195,22 +186,23 @@ def rank_program(g, core, T, topo):
         return lambda: g.iota(out, pattern, base, cm)
 
     col = lambda j: T.col[:, j:j + 1]
-    ICOL, HCOL, T1, T2 = 0, 4, 8, 12
-    CX, CZ = 0, 100
-    ktol = T.ct[:, CZ + 96:CZ + 97]
+    ICOL, HCOL, T1, T2, T3, KT, KT2 = 0, 4, 8, 12, 13, 16, 20
+    CX, CZ, KR = 0, 72, 65
+    ktol = col(KT)
 
-    def cam_load(q):
-        op("sync", lambda: S.dma_start(T.winc[16 * q:16 * q + 16, 0:4096], T.cam[:]), w=["winc%d" % q], tok=("dc", 128), dma=True)
+    def cam_load(q, after):
+        op("sync", lambda: S.dma_start(T.winc[16 * q:16 * q + 16, 0:4096], T.cam[:]), r=after, w=["winc%d" % q], tok=("dc", 128), dma=True)
 
     op("sync", lambda: S.dma_start(T.lensi[:], T.lens[:]), w=["lensi"], tok=("dl", 16), dma=True)
     op("act", lambda: A.dma_start(T.posei[0:8, 0:6], T.pose[:]), w=["posei"], tok=("dp", 16), dma=True)
-    for q in range(CUT["early"]):
-        cam_load(q)
     op("dve", lambda: V.memset(T.winl[:, 0:1024], 8192.0), w=["wl0"])
     op("dve", lambda: V.memset(T.kk[:, :], 0.0), w=["kk", "kk0", "kk32", "kk64"])
-    op("dve", lambda: V.memset(T.ct[:, :], 0.0), w=["ct", "cta", "ctb", "ctc", "ctd", "cte", "ktol"])
+    for q in range(CUT["early"]):
+        cam_load(q, ["kk"])
+    op("dve", lambda: V.memset(T.ct[:, :], 0.0), w=["ct", "cta", "ctb", "ctc", "ctd", "cte"])
     op("act", act(T.winl[:, 3104:WL], T.winl[:, 0:1024], AF.Copy), r=["wl0"], w=["wl2"])
-    op("dve", lambda: V.memset(T.winl[:, 1024:3104], 8192.0), w=["wl1"])
+    op("act", act(T.winl[:, 2656:3104], T.winl[:, 0:448], AF.Copy), r=["wl0"], w=["wl3"])
+    op("dve", lambda: V.memset(T.winl[:, 1024:2656], 8192.0), w=["wl1"])
     op("pool", iota(T.d16[:, :], [[-1, 16]], 0, 1, False), w=["d16"])
     op("pool", iota(T.ones[:, :], [[0, 128]], 1, 0, True), w=["ones"])
     op("pool", lambda: g.affine_select(T.rep[0:8, :], T.ones[0:8, :], [[1, 8], [0, 16]], ALU.is_equal, 0.0, 0, -1), r=["ones"], w=["rep"])
@@ -225,50 +217,52 @@ def rank_program(g, core, T, topo):
             for t in range(4):
                 op("pool", iota(T.kk[32:33, 128 * h + 32 * t:128 * h + 32 * t + 32], [[1, 8], [0, 4]], 8 * own[t], 0, True),
                    r=["kk32"], w=["kk32_%d" % h])
-    op("dve", ts(T.d16a[:, :], T.d16[:, :], 15, None, ALU.bitwise_and), r=["d16"], w=["d16a"])
     op("dve", lambda: V.tensor_copy(T.posef[0:8, 0:6], T.posei[0:8, 0:6]), r=["posei"], w=["posef"])
-    op("dve", lambda: V.tensor_copy(col(ICOL), T.d16a[:, 0:1]), r=["d16a"], w=["icol"])
+    op("dve", ts(T.d16a[:, :], T.d16[:, :], 15, None, ALU.bitwise_and), r=["d16"], w=["d16a"])
     op("pe", mms([(T.p6[:, 0:6], T.rep[0:8, :], T.posef[0:8, 0:6], True, True)]), r=["rep", "posef"], b=["p6"])
+    op("dve", lambda: V.tensor_copy(col(ICOL), T.d16a[:, 0:1]), r=["d16a"], w=["icol"])
     op("dve", lambda: V.tensor_copy(T.hi[:, :], T.lensi[:, :]), r=["lensi"], w=["hi"])
     op("act", act(col(HCOL), T.p6[:, 4:5], AF.Identity, scale=2.0 ** -12), w=["hcol"], b=["p6"])
     op("act", act(T.ct[:, CX:CX + 33:32], T.p6[:, 0:2], AF.Copy), w=["cta"], b=["p6"])
     op("act", act(T.ct[:, CZ:CZ + 1], T.p6[:, 1:2], AF.Identity, scale=-1.0), w=["ctb"], b=["p6"])
-    op("act", act(col(T1), T.p6[:, 2:3], AF.Identity, bias=-15.5 / 8, scale=0.125), w=["t1"], b=["p6"])
     op("act", act(col(T2), T.p6[:, 3:4], AF.Identity, bias=16 - 3.5 / 8, scale=0.125), w=["t2"], b=["p6"])
-    op("act", act(col(T2 + 1), T.p6[:, 5:6], AF.Relu, bias=4095.0, scale=-1.0), w=["t3"], b=["p6"])
+    op("act", act(col(T1), T.p6[:, 2:3], AF.Identity, bias=-15.5 / 8, scale=0.125), w=["t1"], b=["p6"])
     op("act", act(T.ct[:, CZ + 32:CZ + 33], T.p6[:, 0:1], AF.Copy), w=["ctc"], b=["p6"])
-    op("act", act(T.ct[:, CX + 64:CX + 65], col(ICOL), AF.Identity, bias=col(T1), scale=T.ct[:, CX:CX + 1]), r=["icol", "t1", "cta"], w=["ctd"])
     op("act", act(T.ct[:, CZ + 64:CZ + 65], col(ICOL), AF.Identity, bias=col(T2), scale=T.ct[:, CZ:CZ + 1]), r=["icol", "t2", "ctb"], w=["cte"])
-    op("act", act(ktol, col(T2 + 1), AF.Identity, bias=4095.0 * 4096, scale=-4096.0), r=["t3"], w=["ktol"])
-    op("sync", lambda: S.dma_start(T.winl[0:128:16, 16:4112], T.hi[:, :]), r=["hi", "wl0", "wl1", "wl2"], w=["wlhi"], tok=("dw", 48), dma=True)
-    op("dve", ts(T.vi[:, :], T.lensi[:, :], col(HCOL), 15.5 + 2.0 ** -13, ALU.mult, ALU.add), r=["lensi", "hcol"], w=["vi"])
+    op("act", act(T.ct[:, CX + 64:CX + 65], col(ICOL), AF.Identity, bias=col(T1), scale=T.ct[:, CX:CX + 1]), r=["icol", "t1", "cta"], w=["ctd"])
+    op("act", act(col(T3), T.p6[:, 5:6], AF.Relu, bias=4095.0, scale=-1.0), w=["t3"], b=["p6"])
+    op("sync", lambda: S.dma_start(T.winl[0:128:16, 16:4112], T.hi[:, :]), r=["hi", "wl0", "wl1", "wl2", "wl3"], w=["wlhi"], tok=("dw", 48), dma=True)
     op("dve", tt(T.lo[:, 0:128], T.lensi[:, 0:128], T.hi[:, 0:128], ALU.subtract), r=["lensi", "hi"], w=["lo0"])
+    op("dve", ts(T.vi[:, :], T.lensi[:, :], col(HCOL), 15.5 + 2.0 ** -13, ALU.mult, ALU.add), r=["lensi", "hcol"], w=["vi"])
+    op("dve", tt(T.lo[:, 128:192], T.lensi[:, 128:192], T.hi[:, 128:192], ALU.subtract), r=["lensi", "hi"], w=["lo1"])
     op("dve", ts(T.va[:, :], T.vi[:, :], 0x7FFFFFFF, None, ALU.bitwise_and), r=["vi"], w=["va"])
-    op("dve", tt(T.lo[:, 128:256], T.lensi[:, 128:256], T.hi[:, 128:256], ALU.subtract), r=["lensi", "hi"], w=["lo1"])
-    op("sync", lambda: S.dma_start(T.winl[1:128:16, 16:4112], T.lo[:, :]), r=["lo0", "lo1"], w=["wllo"], tok=("dw", 48), dma=True)
+    op("dve", tt(T.lo[:, 192:256], T.lensi[:, 192:256], T.hi[:, 192:256], ALU.subtract), r=["lensi", "hi"], w=["lo2"])
+    op("sync", lambda: S.dma_start(T.winl[1:128:16, 16:4112], T.lo[:, :]), r=["lo0", "lo1", "lo2"], w=["wllo"], tok=("dw", 48), dma=True)
     op("dve", ts(T.vt[:, :], T.va[:, :], 128.0, None, ALU.mult), r=["va"], w=["vt"])
     op("sync", lambda: S.dma_start(T.winl[2:128:16, 16:4112], T.vt[:, :]), r=["vt"], w=["wlvt"], tok=("dw", 48), dma=True)
-    for q in range(CUT["early"], 8):
-        cam_load(q)
     op("dve", lambda: V.memset(T.kk[64:65, :], 1.0), w=["kk64"])
     op("dve", lambda: V.memset(T.ones2[:, :], 1.0), w=["ones2"])
+    for q in range(CUT["early"], 8):
+        cam_load(q, ["ones2"])
     op("pool", lambda: g.affine_select(T.pm[:, :], T.ones2[:, :], [[-1, 16], [-16, 8], [1000, 2]], ALU.is_equal, 0.0, 0, 1), r=["ones2"], w=["pm"])
     op("pool", iota(T.e16i[:, :], [[0, 16], [-1, 16]], 0, 1, False), w=["e16i"])
     op("pool", iota(T.bndc[:, 0:2], [[-62, 2]], 31, 0, True), w=["bndc"])
     op("pool", lambda: g.affine_select(T.bnd[:, 0:1], T.bndc[:, 0:1], [[0, 1]], ALU.is_ge, 31.0 / 512, 15, -1), r=["bndc"], w=["bnd0"])
     op("pool", lambda: g.affine_select(T.bnd[:, 4:5], T.bndc[:, 1:2], [[0, 1]], ALU.is_ge, -31.0 / 512, 15, -1), r=["bndc"], w=["bnd1"])
-    ctall = ["ct", "cta", "ctb", "ctc", "ctd", "cte", "ktol"]
-    op("pe", mms([(T.p7[0:97, 0:128], T.ct[:, CX:CX + 97], T.id32[:, :], True, True),
-                  (T.p7[0:97, 128:256], T.ct[:, CZ:CZ + 97], T.id32[:, :], True, True)]), r=ctall + ["id32"], b=["p7"])
-    op("act", act(T.pt[0:97, :], T.p7[0:97, 0:256], AF.Copy), w=["pt"], b=["p7"])
+    op("pe", mms([(T.p7[0:KR, 128:256], T.ct[:, CZ:CZ + KR], T.id32[:, :], True, True),
+                  (T.p7[0:KR, 0:128], T.ct[:, CX:CX + KR], T.id32[:, :], True, True)]),
+       r=["ct", "cta", "ctb", "ctc", "ctd", "cte", "id32"], b=["p7"])
+    op("act", act(ktol, col(T3), AF.Identity, bias=4095.0 * 4096, scale=-4096.0), r=["t3"], w=["ktol"])
+    op("act", act(col(KT2), col(T3), AF.Identity, bias=4095.0 * 4096 - 128, scale=-4096.0), r=["t3"], w=["ktol2"])
+    op("act", act(T.pt[0:KR, :], T.p7[0:KR, 0:256], AF.Copy), w=["pt"], b=["p7"])
     kkall = ["kk", "kk0", "kk32_0", "kk32_1", "kk64"]
 
     def z_base(h, stop):
-        op("pe", mms([(T["pa%d" % h][:, 0:128], T.pt[0:97, 128:256], T.kk[0:97, 128 * h:128 * h + 128], True, stop)]),
+        op("pe", mms([(T["pa%d" % h][:, 0:128], T.pt[0:KR, 128:256], T.kk[0:KR, 128 * h:128 * h + 128], True, stop)]),
            r=kkall + ["pt"], b=["pa%d" % h])
 
     def x_base(h, stop):
-        op("pe", mms([(T["pb%d" % h][:, 256:384], T.kk[0:97, 128 * h:128 * h + 128], T.pt[0:97, 0:128], True, stop)]),
+        op("pe", mms([(T["pb%d" % h][:, 256:384], T.kk[0:KR, 128 * h:128 * h + 128], T.pt[0:KR, 0:128], True, stop)]),
            r=kkall + ["pt"], b=["pb%d" % h])
 
     def a_zo(p, h):
@@ -283,7 +277,7 @@ def rank_program(g, core, T, topo):
         n = "%d%d" % (p, h)
         op("act", act(T["nz" + n][:, :], T["pa%d" % h][:, 0:128], AF.Identity, bias=-MAGIC, scale=-1.0), w=["nz" + n], b=["pa%d" % h])
 
-    wl = ["wl0", "wl1", "wl2", "wlhi", "wllo", "wlvt"]
+    wl = ["wl0", "wl1", "wl2", "wl3", "wlhi", "wllo", "wlvt"]
     wc = ["winc%d" % q for q in range(8)] + ["wcz"]
     gall = lambda out, k0=0, k1=128: ["%s_%d" % (out, k) for k in range(k0, k1, 2)]
 
@@ -316,47 +310,38 @@ def rank_program(g, core, T, topo):
     def x_lens(p, h):
         n = "%d%d" % (p, h)
         pb, gl = T["pb%d" % h], T["gl" + n]
-        op("pe", mms([(pb[:, i:256:16], gl[:, i:2048:16], T.sell[:, :], p == 1, p == 1 or i == 15) for i in range(16)]),
+        op("pe", mms([(pb[:, i:256:16], gl[:, i:2048:16], T.sell[:, :], True, True) for i in range(16)]),
            r=gall("gl" + n) + ["sell0", "sell1"], b=["pb%d" % h])
-
-    def ktol_start(h):
-        op("pe", mms([(T["pb%d" % h][:, 0:256], T.s96[0:97, :], T.pt[0:97, :], True, False)]), r=["s96", "pt"], b=["pb%d" % h])
 
     def b_steps(p, h):
         n = "%d%d" % (p, h)
-        pa, pb = T["pa%d" % h], T["pb%d" % h]
+        pa, pb, pc, pen = T["pa%d" % h], T["pb%d" % h], T["pc%d" % h], T["pen" + n]
 
         def b1():
             op("dve", tt(T["w" + n][:, :], T["xi" + n][:, :], pb[:, 0:128], ALU.mult), r=["xi" + n], w=["w" + n], b=["pb%d" % h])
+            op("act", act(T["vb" + n][:, :], pb[:, 128:256], AF.Copy), w=["vb" + n], b=["pb%d" % h])
+            op("act", act(T["q" + n][:, :], T["w" + n][:, :], AF.Abs, bias=0.5, scale=4096.0), r=["w" + n], w=["q" + n])
 
         def b2():
-            op("dve", ts(T["ui" + n][:, :], T["w" + n][:, :], 2.0 ** -12, 63.5 + 2.0 ** -13, ALU.mult, ALU.add), r=["w" + n], w=["ui" + n])
+            op("dve", ts(T["ub" + n][:, :], T["w" + n][:, :], 191.5 + 2.0 ** -13, 128.0, ALU.add, ALU.max), r=["w" + n], w=["ub" + n])
+            op("pe", mms([(pa[:, 128:256], T["ub" + n][:, :], T.idbf[:, :], True, False),
+                          (pa[:, 128:256], T["vb" + n][:, :], T.idbf[:, :], False, True)]), r=["vb" + n, "ub" + n, "idbf"], b=["pa%d" % h])
 
         def b3():
-            op("dve", tt(T["s" + n][:, :], T["ui" + n][:, :], pb[:, 128:256], ALU.add), r=["ui" + n], w=["s" + n], b=["pb%d" % h])
-            op("pe", mms([(pa[:, 128:256], T["s" + n][:, :], T.id32[:, :], True, True)]), r=["s" + n, "id32"], b=["pa%d" % h])
+            op("dve", ts(T["po" + n][:, :], pa[:, 128:256], 128.0, 4096.0, ALU.subtract, ALU.min), w=["po" + n], b=["pa%d" % h])
 
         def b4():
+            op("act", act(pen[:, :], T["q" + n][:, :], AF.Relu, bias=-(2.0 ** 35), scale=2.0 ** 17), r=["q" + n], w=["pen" + n])
             if p == 1:
-                op("dve", ts(T["po" + n][:, :], pa[:, 128:256], 4096.0, None, ALU.min), w=["po" + n], b=["pa%d" % h])
+                op("pe", mms([(pc[:, 2 * x:256:16], T.idbf[:, :], pen[:, 16 * x:16 * x + 16], False, False) for x in range(8)]),
+                   r=["pen" + n, "idbf"], b=["pc%d" % h])
             else:
-                op("dve", ts(T["po" + n][:, :], pa[:, 128:256], ktol, 4096.0, ALU.subtract, ALU.min), r=["ktol"], w=["po" + n], b=["pa%d" % h])
+                a_nz(p, h)
+                op("act", act(T["sn%d" % h][:, :], pa[:, 128:256], AF.Identity, bias=col(KT2)), r=["ktol2"], w=["sn%d" % h], b=["pa%d" % h])
+                op("pe", mms([(pc[:, 0:128], T["nz" + n][:, :], T.id32[:, :], True, False), (pc[:, 0:128], T.idbf[:, :], pen[:, :], False, False)]),
+                   r=["pen" + n, "idbf", "id32", "nz" + n], b=["pc%d" % h])
         c = CUT["b"]
-        return [("v", c[0]), ("a", None), b1, ("v", c[1]), b2, ("v", c[2]), b3, ("v", c[3]), b4]
-
-    def b_pen(p, h):
-        n = "%d%d" % (p, h)
-        pc, pen = T["pc%d" % h], T["pen" + n]
-        op("act", act(T["q" + n][:, :], T["w" + n][:, :], AF.Abs, bias=0.5), r=["w" + n], w=["q" + n])
-        if p == 2:
-            a_nz(p, h)
-        op("act", act(pen[:, :], T["q" + n][:, :], AF.Relu, bias=-(2.0 ** 35), scale=2.0 ** 17), r=["q" + n], w=["pen" + n])
-        if p == 1:
-            op("pe", mms([(pc[:, 2 * x:256:16], T.idbf[:, :], pen[:, 16 * x:16 * x + 16], False, False) for x in range(8)]),
-               r=["pen" + n, "idbf"], b=["pc%d" % h])
-        else:
-            op("pe", mms([(pc[:, 0:128], T["nz" + n][:, :], T.id32[:, :], True, False), (pc[:, 0:128], T.idbf[:, :], pen[:, :], False, False)]),
-               r=["pen" + n, "idbf", "id32", "nz" + n], b=["pc%d" % h])
+        return [("v", c[0]), ("a", CUT["ba"]), b1, ("a", None), ("v", c[1]), b2, ("v", c[2]), b3, ("v", c[3])], b4
 
     def x_depth(p, h):
         n = "%d%d" % (p, h)
@@ -368,9 +353,12 @@ def rank_program(g, core, T, topo):
         op("pe", mms(lst), r=gall("gd" + n) + ["seld0", "seld1"], b=["pc%d" % h])
 
     def c_abs(p, h):
-        pc = T["pc%d" % h]
-        op("act", act(pc[:, 256:384], pc[:, 0:256:2] if p == 1 else pc[:, 0:128], AF.Abs, bias=4096.0 * (MAGIC + 16), scale=4096.0),
-           b=["pc%d" % h])
+        pa, pc = T["pa%d" % h], T["pc%d" % h]
+        if p == 1:
+            op("act", act(pc[:, 256:384], pc[:, 0:256:2], AF.Abs, bias=4096.0 * (MAGIC + 16), scale=4096.0), b=["pc%d" % h])
+        else:
+            op("act", act(T["ab%d" % h][:, :], pc[:, 0:128], AF.Abs, bias=4096.0 * (MAGIC + 16), scale=4096.0), w=["ab%d" % h], b=["pc%d" % h])
+            op("pe", mms([(pa[:, 256:384], T["ab%d" % h][:, :], T.id32[:, :], True, True)]), r=["ab%d" % h, "id32"], b=["pa%d" % h])
 
     def c_sums(h):
         pc, sc, snd = T["pc%d" % h], T["sc%d" % h], T["snd%d" % h]
@@ -395,9 +383,9 @@ def rank_program(g, core, T, topo):
 
         def f():
             tr = [RemoteDMATransfer(dst_ids=[dst_id(r) for r in grp], dma_engine_mask=m, remote_sem=sem,
-                                    srcs=[snd], dsts=[land for _r in grp]) for grp, m in ((far, moff), (near, mon))]
+                                    srcs=[snd], dsts=[land for _r in grp]) for grp, m in ((far, moff), (near, mon[h]))]
             return g.remote_dma_fused(tr, local_sem=T.sem.ls)
-        left[0] += _count(moff) + _count(mon)
+        left[0] += noff + HOME[h]
         op("pool", f, r=["sna%d" % h, "snb%d" % h], tok=("ls", 0))
 
     def shift_own(h):
@@ -406,7 +394,7 @@ def rank_program(g, core, T, topo):
 
     def shift_sum(h):
         pa, pb, pc, sh = T["pa%d" % h], T["pb%d" % h], T["pc%d" % h], T["sh%d" % h]
-        op("ext", None, w=["rcv%d" % h], tok=("xa%d" % h, arrive))
+        op("ext", None, w=["rcv%d" % h], tok=("xa%d" % h, sum(incs(r, h) for r in others)))
         op("pe", mms([(pc[0:32, 384:512], T["rcv%d" % h][:, r, :], T.idbf[:, :], False, r == others[-1]) for r in others]),
            r=["rcv%d" % h], b=["pc%d" % h])
         op("dve", ts(sh[:, :], pc[0:32, 384:512], T.bnd[:, 4:5], T.bnd[:, 0:1], ALU.max, ALU.min), r=["bnd0", "bnd1"], w=["sh%d" % h], b=["pc%d" % h])
@@ -414,12 +402,10 @@ def rank_program(g, core, T, topo):
         op("pe", mms([(pb[:, 256:384], sh[:, :], T.ww[:, 0:128], False, True)]), r=["ww", "sh%d" % h], b=["pb%d" % h])
 
     def c_keep(h):
-        pa, pc = T["pa%d" % h], T["pc%d" % h]
-        op("dve", tt(T["mk%d" % h][:, :], T["s2%d" % h][:, :], pc[:, 256:384], ALU.max), r=["s2%d" % h], w=["mk%d" % h], b=["pc%d" % h])
-        op("pe", mms([(pa[:, 256:384], T["mk%d" % h][:, :], T.id32[:, :], True, True)]), r=["mk%d" % h, "id32"], b=["pa%d" % h])
+        op("dve", tt(T["kp%d" % h][:, :], T["sn%d" % h][:, :], T["pa%d" % h][:, 256:384], ALU.max), r=["sn%d" % h], w=["kp%d" % h], b=["pa%d" % h])
 
     def c_off(h):
-        op("dve", ts(T["fo%d" % h][:, :], T["pa%d" % h][:, 256:384], ktol, 4096.0, ALU.subtract, ALU.min), r=["ktol"], w=["fo%d" % h], b=["pa%d" % h])
+        op("dve", ts(T["fo%d" % h][:, :], T["kp%d" % h][:, :], ktol, 4096.0, ALU.subtract, ALU.min), r=["ktol", "kp%d" % h], w=["fo%d" % h])
 
     fbank = lambda j: (("pb0", "pc0", "pb1")[j % 3], 64 * (j // 3))
 
@@ -436,9 +422,9 @@ def rank_program(g, core, T, topo):
         src = T.fout[:, b, :]
         op("dve", lambda: V.tensor_copy(src, T[bk][:, c0:c0 + 64]), w=["fout%d" % b], b=[bk])
         if owner != rank:
-            m = moff if owner in far else mon
+            m = moff if owner in far else mon[2]
             rid, pid, _se = topo.addr(cores[owner])
-            left[0] += _count(m)
+            left[0] += noff if owner in far else HOME[2]
             sem = T.sem["fb" if is_late(rank, owner) else "fa"]
             op("pool", lambda: g.remote_dma(T.frecv[:, rank, :], src, sem, T.sem.ls, pid, rid, m), r=["fout%d" % b], tok=("ls", 0))
 
@@ -446,17 +432,18 @@ def rank_program(g, core, T, topo):
     z_base(1, True)
     x_base(0, True)
     x_base(1, True)
-    op("dve", tt(T.sell[:, 0:8], T.id32[:, 0:128:16], T.id32[:, 1:128:16], ALU.add), r=["id32"], w=["sell0"])
+    op("dve", tt(T.selt[:, 8:16], T.id32[:, 0:128:16], T.id32[:, 1:128:16], ALU.add), r=["id32"], w=["selu"])
     op("dve", lambda: V.tensor_copy(T.sell[:, 8:16], T.id32[:, 2:128:16]), r=["id32"], w=["sell1"])
     op("dve", lambda: V.memset(T.winc[:, 4096:WC], 0.0), w=["wcz"])
     op("dve", lambda: V.memset(T.rst[:, :], 1.0), w=["rst"])
-    op("act", act(T.selt[:, :], T.id32[:, 1:128:16], AF.Identity, scale=2.0 ** -9), r=["id32"], w=["selt"])
+    op("dve", ts(T.sell[:, 0:8], T.selt[:, 8:16], 2.0 ** -12, None, ALU.mult), r=["selu"], w=["sell0"])
+    op("act", act(T.selt[:, 0:8], T.id32[:, 1:128:16], AF.Identity, scale=2.0 ** -9), r=["id32"], w=["selt"])
     op("act", act(T.idbf[:, :], T.id32[:, :], AF.Copy), r=["id32"], w=["idbf"])
     op("act", act(T.seld[:, 0:16:2], T.id32[:, 15:128:16], AF.Identity, scale=16.0), r=["id32"], w=["seld0"])
     op("act", act(T.kb[:, :], T.ones[:, :], AF.Identity, scale=ktol), r=["ones", "ktol"], w=["kb"])
-    op("dve", tt(T.seld[:, 1:16:2], T.id32[:, 0:128:16], T.selt[:, :], ALU.add), r=["id32", "selt"], w=["seld1"])
-    op("dve", lambda: V.memset(T.rst[:, 0:128:8], 0.0), w=["rst"])
     a_zo(1, 0)
+    op("dve", tt(T.seld[:, 1:16:2], T.id32[:, 0:128:16], T.selt[:, 0:8], ALU.add), r=["id32", "selt"], w=["seld1"])
+    op("dve", lambda: V.memset(T.rst[:, 0:128:8], 0.0), w=["rst"])
     a_zo(1, 1)
     a_nz(1, 0)
     a_nz(1, 1)
@@ -467,77 +454,82 @@ def rank_program(g, core, T, topo):
         op("pe", mms([(T["pc%d" % h][:, 0:256], T["nz1%d" % h][:, :], T.pm[:, :], True, False)]), r=["nz1%d" % h, "pm"], b=["pc%d" % h])
 
     slot("gl10", "zo10", [("v", CUT["plain"]), ("a", None)])
-    op("act", act(T.tolt[:, :], T.p6[:, 128:256], AF.Copy), w=["tolt"], b=["p6"])
     x_lens(1, 0)
-    slot("gl11", "zo11", b_steps(1, 0))
+    seq, b4 = b_steps(1, 0)
+    slot("gl11", "zo11", seq)
     x_lens(1, 1)
-    b_pen(1, 0)
-    slot("gd10", "po10", b_steps(1, 1))
+    b4()
+    seq, b4 = b_steps(1, 1)
+    slot("gd10", "po10", seq)
     x_depth(1, 0)
+    op("act", act(T.tolt[:, :], T.p6[:, 128:256], AF.Copy), w=["tolt"], b=["p6"])
     c = CUT["c1"]
-    seq = [("v", c[0]), ("a", CUT["c1a"]), lambda: c_abs(1, 0), lambda: b_pen(1, 1), ("a", None)]
+    seq = [("v", c[0]), ("a", CUT["c1a"]), lambda: c_abs(1, 0), b4, ("a", None)]
     steps = c_sums(0)
     for st in steps[:-1]:
         seq += [st, ("v", c[1])] if c[1] else [st]
     slot("gd11", "po11", seq + [steps[-1], lambda: send_shift(0), ("v", c[2])])
     x_depth(1, 1)
     c_abs(1, 1)
-    fill = [lambda: op("dve", lambda: V.memset(T.selw[:, :], 0.0), w=["selw"]),
-            lambda: op("dve", lambda: V.memset(T.s96[:, :], 0.0), w=["s96"]),
-            lambda: op("dve", lambda: V.memset(T.selw[0:1, 0:16], 0.125), r=["selw"], w=["selw0"]),
-            lambda: op("dve", lambda: V.memset(T.selw[32:33, 16:32], 64.0), r=["selw"], w=["selw1"])]
-    for i, st in enumerate(c_sums(1)):
-        st()
-        if i < len(fill):
-            fill[i]()
-    send_shift(1)
+    op("dve", lambda: V.memset(T.selw[:, :], 0.0), w=["selw"])
     op("dve", ts(T.e16a[:, :], T.e16i[:, :], 15, None, ALU.bitwise_and), r=["e16i"], w=["e16a"])
-    op("dve", lambda: V.memset(T.s96[96:97, :], 1.0), w=["s96"])
+    op("dve", ts(T.selc[:, :], T.d16a[:, :], 0.0, None, ALU.is_equal), r=["d16a"], w=["selc"])
+    op("dve", lambda: V.memset(T.selw[0:1, 0:16], 0.125), r=["selw"], w=["selw0"])
+    op("dve", lambda: V.memset(T.selw[32:33, 16:32], 64.0), r=["selw"], w=["selw1"])
+    for st in c_sums(1):
+        st()
+    send_shift(1)
     op("dve", ts(T.e16[:, :], T.e16a[:, :], 0.0, None, ALU.is_equal), r=["e16a"], w=["e16"])
-    op("pe", mms([(T.p7[0:32, 256:512], T.selw[0:97, :], T.pt[0:97, :], True, True)]), r=["selw", "selw0", "selw1", "pt"], b=["p7"])
+    op("pe", mms([(T.p7[0:32, 256:512], T.selw[0:KR, :], T.pt[0:KR, :], True, True)]), r=["selw", "selw0", "selw1", "pt"], b=["p7"])
     for h in range(2):
         z_base(h, False)
         x_base(h, False)
         shift_own(h)
-    op("dve", ts(T.selc[:, :], T.d16a[:, :], 0.0, None, ALU.is_equal), r=["d16a"], w=["selc"])
     op("dve", tt(T.ww[:, :], T.e16[:, :], T.p7[0:32, 256:512], ALU.mult), r=["e16"], w=["ww"], b=["p7"])
     op("dve", lambda: V.tensor_copy(T.id16[:, :], T.id32[:, :]), r=["id32"], w=["id16"])
 
     shift_sum(0)
     a_zo(2, 0)
     c = CUT["x"]
-    slot("gl20", "zo20", [("a", None), lambda: a_x(2, 0), lambda: ktol_start(0), ("v", c[0]), lambda: shift_sum(1), ("v", c[1]),
+    slot("gl20", "zo20", [("a", None), lambda: a_x(2, 0), ("v", c[0]), lambda: shift_sum(1), ("v", c[1]),
                           lambda: a_zo(2, 1), lambda: a_x(2, 1)])
     x_lens(2, 0)
-    ktol_start(1)
-    slot("gl21", "zo21", b_steps(2, 0))
+    seq, b4 = b_steps(2, 0)
+    slot("gl21", "zo21", seq)
     x_lens(2, 1)
-    b_pen(2, 0)
-    slot("gd20", "po20", b_steps(2, 1))
+    b4()
+    seq, b4 = b_steps(2, 1)
+    slot("gd20", "po20", seq)
     x_depth(2, 0)
     c = CUT["c2"]
-    slot("gd21", "po21", [("v", c[0]), ("a", CUT["c2a"]), lambda: c_abs(2, 0), lambda: b_pen(2, 1), ("a", None), lambda: c_keep(0),
+    slot("gd21", "po21", [("v", c[0]), ("a", CUT["c2a"]), lambda: c_abs(2, 0), b4, ("a", None), lambda: c_keep(0),
                           ("v", c[1]), lambda: c_off(0), ("v", c[2])])
     x_depth(2, 1)
     seq = _blocks(topo, cores, perm, rank)
     for j, b in enumerate(seq):
         h, t = divmod(b, 4)
-        gf, fo, k0 = "gf%d" % h, "fo%d" % h, 32 * t
-        gather("act", gf, fo, k0 + CUT["f"], k0 + 32)
-        gather("dve", gf, fo, k0, k0 + CUT["f"])
+        gf, fo, k0, kv = "gf%d" % h, "fo%d" % h, 32 * t, CUT["f"][j]
+        gather("act", gf, fo, k0 + kv, k0 + 32)
+        if j >= 6:
+            gather("dve", gf, fo, k0, k0 + 6)
+            f_out(seq[j - 1], j - 1)
+            gather("dve", gf, fo, k0 + 6, k0 + kv)
+        else:
+            gather("dve", gf, fo, k0, k0 + kv)
+        if j == 2:
+            c_keep(1)
+        if 0 < j < 6:
+            f_out(seq[j - 1], j - 1)
+        if j == 2:
+            c_off(1)
+        f_sum(b, j)
         if j == 0:
             c_abs(2, 1)
-            c_keep(1)
-        f_sum(b, j)
-        if j > 0:
-            f_out(seq[j - 1], j - 1)
-        if j == 1:
-            c_off(1)
     f_out(seq[7], 7)
     op("pe", mms([(T.p6[0:64, 256:384], T.fout[:, seq[7], :], T.id16[:, :], True, False)]), r=["fout%d" % seq[7], "id16"], b=["p6"])
     groups = [(s, grp) for s, grp in (("fa", early), ("fb", late)) if grp]
     for s, grp in groups:
-        op("ext", None, w=[s], tok=(s, sum(incs[r] for r in grp)))
+        op("ext", None, w=[s], tok=(s, sum(incs(r, 2) for r in grp)))
         op("pe", mms([(T.p6[0:64, 256:384], T.frecv[:, r, :], T.id16[:, :], False, s == groups[-1][0] and r == grp[-1]) for r in grp]),
            r=[s], b=["p6"])
     op("dve", lambda: V.tensor_copy(T.yb[:, :], T.p6[0:64, 256:384]), w=["yb"], b=["p6"])

@@ -4,37 +4,34 @@ from concourse.mybir import AluOpType as ALU, ActivationFunctionType as AF
 N = 8
 F32, BF, I32, U16, F16 = "float32", "bfloat16", "int32", "uint16", "float16"
 MAGIC = 12582912.0
-WL, WC = 4128, 4112
+POFF = 128.0 * 192
+WL, WC = 4128, 4240
 
 SCRATCH = {
-    "lensi": ("sbuf", [128, 256], I32), "posei": ("sbuf", [8, 8], I32), "posef": ("sbuf", [8, 8], F32),
+    "lensi": ("sbuf", [128, 256], I32), "posei": ("sbuf", [8, 8], I32), "poseb": ("sbuf", [8, 16], BF),
+    "zo1": ("sbuf", [128, 256], U16), "xi1": ("sbuf", [128, 256], I32),
     "hi": ("sbuf", [128, 256], BF), "lo": ("sbuf", [128, 256], BF), "vt": ("sbuf", [128, 256], BF),
-    "vi": ("sbuf", [128, 256], I32), "va": ("sbuf", [128, 256], I32),
     "winl": ("sbuf", [128, WL], BF), "winc": ("sbuf", [128, WC], BF),
-    "ones": ("sbuf", [128, 128], F32), "rep": ("sbuf", [8, 128], F32), "id32": ("sbuf", [128, 128], F32),
-    "ones2": ("sbuf", [128, 256], F32), "pm": ("sbuf", [128, 256], F32), "kb": ("sbuf", [128, 128], F32),
-    "rst": ("sbuf", [128, 128], F32),
+    "rep": ("sbuf", [8, 128], BF), "pm": ("sbuf", [128, 128], BF), "rst": ("sbuf", [128, 128], BF),
     "idbf": ("sbuf", [128, 128], BF), "id16": ("sbuf", [128, 128], F16),
-    "d16": ("sbuf", [128, 16], I32), "d16a": ("sbuf", [128, 16], I32),
-    "e16i": ("sbuf", [32, 256], I32), "e16a": ("sbuf", [32, 256], I32), "e16": ("sbuf", [32, 256], F32),
-    "sell": ("sbuf", [128, 16], BF), "seld": ("sbuf", [128, 16], BF), "selc": ("sbuf", [128, 16], BF),
-    "selt": ("sbuf", [128, 16], F32),
-    "col": ("sbuf", [128, 24], F32), "ct": ("sbuf", [128, 144], F32), "pt": ("sbuf", [128, 256], F32),
-    "kk": ("sbuf", [128, 256], F32), "selw": ("sbuf", [128, 32], F32),
-    "ww": ("sbuf", [32, 256], BF), "tolt": ("sbuf", [128, 128], F32),
-    "bndc": ("sbuf", [32, 8], F32), "bnd": ("sbuf", [32, 8], F32),
+    "d16": ("sbuf", [128, 16], I32), "d16a": ("sbuf", [128, 16], I32), "ii": ("sbuf", [128, 2], I32),
+    "wsc": ("sbuf", [32, 12], F32), "wt": ("sbuf", [128, 48], BF),
+    "sel": ("sbuf", [128, 48], BF), "selc": ("sbuf", [128, 16], BF),
+    "col": ("sbuf", [128, 8], F32), "ct": ("sbuf", [128, 176], BF), "pt": ("sbuf", [128, 384], BF),
+    "kk": ("sbuf", [128, 256], BF), "kn": ("sbuf", [128, 256], BF), "kx": ("sbuf", [32, 256], BF), "ww": ("sbuf", [32, 384], BF),
     "frecv": ("sbuf", [128, N, 64], F16), "fout": ("sbuf", [128, N, 64], F16), "yb": ("sbuf", [64, 128], F32),
 }
 for _h in range(2):
-    for _n in ("mk", "mv", "sc", "sn", "ab", "kp"):
+    for _n in ("ab", "mk", "mv", "sc"):
         SCRATCH["%s%d" % (_n, _h)] = ("sbuf", [128, 128], F32)
+    SCRATCH["gb%d" % _h] = ("sbuf", [128, 256], BF)
     SCRATCH["snd%d" % _h] = ("sbuf", [128, 32], BF)
     SCRATCH["rcv%d" % _h] = ("sbuf", [128, N, 32], BF)
     SCRATCH["sh%d" % _h] = ("sbuf", [32, 128], BF)
     SCRATCH["fo%d" % _h] = ("sbuf", [128, 128], U16)
     SCRATCH["gf%d" % _h] = ("sbuf", [128, 2048], BF)
     for _p in (1, 2):
-        for _n, _d in (("zo", U16), ("po", U16), ("xi", I32), ("ub", BF), ("vb", BF), ("nz", F32), ("w", F32), ("q", F32), ("pen", BF)):
+        for _n, _d in (("zo", U16), ("po", U16), ("xi", I32), ("ub", BF), ("vb", BF), ("w", F32), ("q", F32), ("pen", BF)):
             SCRATCH["%s%d%d" % (_n, _p, _h)] = ("sbuf", [128, 128], _d)
         SCRATCH["gl%d%d" % (_p, _h)] = ("sbuf", [128, 2048], BF)
         SCRATCH["gd%d%d" % (_p, _h)] = ("sbuf", [128, 2048], BF)
@@ -43,11 +40,24 @@ for _h in range(2):
 SCRATCH["p6"] = ("psum", [128, 512], F32)
 SCRATCH["p7"] = ("psum", [128, 512], F32)
 
-SEMAPHORES = ["pe", "dve", "act", "pool", "dl", "dp", "dw", "dc", "dy", "xa0", "xa1", "fa", "fb", "ls"]
+SEMAPHORES = ["pe", "dve", "act", "pool", "dl", "dp", "dw", "dc", "dy", "xa0", "xa1", "xb0", "xb1", "fa", "fb", "ls"]
 
-CUT = {"early": 3, "plain": 62, "b": (30, 6, 18, 10), "ba": 40, "c1": (30, 4, 12), "c1a": 20, "x": (48, 10), "c2": (48, 6, 8), "c2a": 24,
-       "f": (14, 22, 12, 14, 14, 14, 14, 14), "late": 5}
-HOME = (4, 4, 4)
+CUT = {"first": 4, "fill": (640, 640, 640, 512), "gate": "zo10", "early": 2, "late": 5}
+PLAN = """
+more4 v:gl10:58 a:gl10 lens10
+v:gl11:48 a:gl11:54 w10 row10 q10 u10 turn10 v:gl11:16 a:gl11 off10 lens11 pen10
+v:gd10:32 a:gd10:40 w11 row11 u11 turn11 a:gd10:26 v:gd10 depth10 off11 q11 pen11
+v:gd11:28 a:gd11:8 abs0 a:gd11:66 sum0 sum0 sum0 sum0 sum0 send0 v:gd11 more0 base0 depth11 more2 weights0 abs1 weights1 more1 weights2
+sum1 sum1 sum1 sum1 sum1 send1 more3 base1 own0
+add0 clamp0 z20 a:gl20:74 x20 own1 test0 add1 v:gl20:48 clamp1 v:gl20 z21 lens20
+v:gl21:36 a:gl21:56 w20 x21 row20 q20 a:gl21:14 test1 u20 turn20 v:gl21:20 off20 v:gl21 lens21 pen20
+v:gd20:40 a:gd20:50 w21 row21 a:gd20:18 q21 u21 turn21 v:gd20:20 off21 v:gd20 depth20
+v:gd21:50 a:gd21:44 fail0 pen21 a:gd21:10 v:gd21 last0 depth21
+a:b0:18 v:b0 a:b1:6 fold0 fail1 v:b1 out0 fold1 a:b2:24 v:b2 last1 out1 fold2
+a:b3:8 v:b3 out2 fold3 a:b4:22 v:b4 out3 fold4 a:b5:18 v:b5 out4 fold5
+a:b6:22 v:b6:10 out5 v:b6 fold6 a:b7:18 v:b7:4 out6 v:b7 fold7 out7
+"""
+HOME = (2, 2)
 
 
 def _masks(topo, cores, src):
@@ -59,13 +69,12 @@ def _masks(topo, cores, src):
 
 
 def _blocks(topo, cores, perm, rank):
-    seq, homes = [], []
-    for h in range(2):
-        home = [t for t in range(4) if topo.chip(cores[perm[4 * h + t]]) == topo.chip(cores[rank])][0]
-        seq += [4 * h + (home + d) % 4 for d in (1, 2, 3)]
-        homes.append(4 * h + home)
+    chip = lambda b: topo.chip(cores[perm[b]])
     mine = perm.index(rank)
-    return seq + [b for b in homes if b != mine] + [mine]
+    seq = []
+    for h in range(2):
+        seq += [b for b in (4 * h + (mine + d) % 4 for d in (1, 2, 3, 4)) if chip(b) != chip(mine)]
+    return seq + [b for b in range(N) if b not in seq and b != mine] + [mine]
 
 
 def _emit(g, T, ops):
@@ -77,8 +86,8 @@ def _emit(g, T, ops):
     for o in ops:
         deps = []
         for r in o["r"]:
-            if r in last_w:
-                deps.append(last_w[r])
+            assert r in last_w, r
+            deps.append(last_w[r])
         for w in o["w"]:
             if w in last_w:
                 deps.append(last_w[w])
@@ -137,16 +146,15 @@ def rank_program(g, core, T, topo):
     if rank is None:
         return
     cores = list(T.cores)
-    by_chip = {}
-    for r, c in enumerate(cores):
-        by_chip.setdefault(topo.chip(c), []).append(r)
-    perm = [rs[0] for rs in by_chip.values()] + [rs[1] for rs in by_chip.values()]
+    perm = list(range(0, N, 2)) + list(range(1, N, 2))
     moff, noff, rest = _masks(topo, cores, core)
     mon = [sum(1 << e for e in rest[:n]) for n in HOME]
     others = [r for r in range(N) if r != rank]
     near = [r for r in others if topo.chip(cores[r]) == topo.chip(core)]
-    far = [r for r in others if r not in near]
-    incs = lambda r, step: HOME[step] if r in near else _masks(topo, cores, cores[r])[1]
+    far_of = lambda s: sorted((r for r in range(N) if topo.chip(cores[r]) != topo.chip(cores[s])), key=lambda r: (r - s) % N)
+    far = far_of(rank)
+    second_call = lambda src, dst: dst in far_of(src)[CUT["first"]:]
+    incs = lambda r, step: HOME[step] if r in near and step < 2 else _masks(topo, cores, cores[r])[1]
     is_late = lambda src, dst: _blocks(topo, cores, perm, src).index(perm.index(dst)) >= CUT["late"]
     late = [r for r in others if is_late(r, rank)]
     early = [r for r in others if r not in late]
@@ -155,10 +163,7 @@ def rank_program(g, core, T, topo):
     ops = []
 
     def op(e, f, r=(), w=(), b=(), tok=None, dma=False):
-        w = list(w)
-        if e == "pool" and tok is None:
-            w.append("q7")
-        ops.append({"e": e, "f": f, "r": list(r), "w": w, "b": list(b), "tok": tok, "dma": dma,
+        ops.append({"e": e, "f": f, "r": list(r), "w": list(w), "b": list(b), "tok": tok, "dma": dma,
                     "used": False, "n": len(ops)})
 
     def ts(out, in0, s1, s2, o0, o1=None):
@@ -185,106 +190,123 @@ def rank_program(g, core, T, topo):
             return lambda: g.iota(out, pattern, base, cm, allow_small_or_imprecise_dtypes=True)
         return lambda: g.iota(out, pattern, base, cm)
 
-    col = lambda j: T.col[:, j:j + 1]
-    ICOL, HCOL, T1, T2, T3, KT, KT2 = 0, 4, 8, 12, 13, 16, 20
-    CX, CZ, KR = 0, 72, 65
-    ktol = col(KT)
+    CX, CZ, KB, KR = 0, 72, 72, 99
+    sell, seld, sele = T.sel[:, 0:16], T.sel[:, 16:32], T.sel[:, 32:48]
+    zeros = T.winc[:, 0:128]
+
+    def mark(out, name, pattern, base, cm, value=1.0, src=None, test=ALU.not_equal, after=("wcy",)):
+        n = 1
+        for _step, count in pattern:
+            n *= count
+        src = T.winc[0:out.shape[0], 0:n] if src is None else src
+        op("pool", lambda: g.affine_select(out, src, pattern, test, value, base, cm), r=after, w=[name])
 
     def cam_load(q, after):
-        op("sync", lambda: S.dma_start(T.winc[16 * q:16 * q + 16, 0:4096], T.cam[:]), r=after, w=["winc%d" % q], tok=("dc", 128), dma=True)
+        op("sync", lambda: S.dma_start(T.winc[16 * q:16 * q + 16, 128:4224], T.cam[:]), r=after, w=["winc%d" % q], tok=("dc", 128), dma=True)
 
+    ctall = ["ct%d" % k for k in range(9)]
     op("sync", lambda: S.dma_start(T.lensi[:], T.lens[:]), w=["lensi"], tok=("dl", 16), dma=True)
     op("act", lambda: A.dma_start(T.posei[0:8, 0:6], T.pose[:]), w=["posei"], tok=("dp", 16), dma=True)
-    op("dve", lambda: V.memset(T.winl[:, 0:1024], 8192.0), w=["wl0"])
-    op("dve", lambda: V.memset(T.kk[:, :], 0.0), w=["kk", "kk0", "kk32", "kk64"])
+    op("dve", lambda: V.memset(zeros, 0.0), w=["wcy"])
+    op("dve", lambda: V.memset(T.winl[:, 0:CUT["fill"][0]], 0.0), w=["wl0"])
     for q in range(CUT["early"]):
-        cam_load(q, ["kk"])
-    op("dve", lambda: V.memset(T.ct[:, :], 0.0), w=["ct", "cta", "ctb", "ctc", "ctd", "cte"])
-    op("act", act(T.winl[:, 3104:WL], T.winl[:, 0:1024], AF.Copy), r=["wl0"], w=["wl2"])
-    op("act", act(T.winl[:, 2656:3104], T.winl[:, 0:448], AF.Copy), r=["wl0"], w=["wl3"])
-    op("dve", lambda: V.memset(T.winl[:, 1024:2656], 8192.0), w=["wl1"])
+        cam_load(q, ["wl0"])
+    fill, end = ["wl0", "wl1"], WL
+    for k, n in enumerate(CUT["fill"][1:]):
+        op("act", act(T.winl[:, end - n:end], T.winl[:, 0:n], AF.Copy), r=["wl0"], w=["wl%d" % (k + 2)])
+        fill, end = fill + ["wl%d" % (k + 2)], end - n
+    op("dve", lambda: V.memset(T.winl[:, CUT["fill"][0]:end], 0.0), w=["wl1"])
+
+    def table(r, src, name):
+        op("sync", lambda: S.dma_start(T.winl[r:128:16, 16:4112], src[:, :]), r=[name] + fill, w=["wl" + name], tok=("dw", 48), dma=True)
+
+    op("dve", lambda: V.memset(T.ct[:, :], 0.0), w=["ct"] + ctall)
+    op("dve", lambda: V.memset(T.ct[:, CZ + 70:CZ + KR:28], -7.0 / 16), w=["ct0"])
     op("pool", iota(T.d16[:, :], [[-1, 16]], 0, 1, False), w=["d16"])
-    op("pool", iota(T.ones[:, :], [[0, 128]], 1, 0, True), w=["ones"])
-    op("pool", lambda: g.affine_select(T.rep[0:8, :], T.ones[0:8, :], [[1, 8], [0, 16]], ALU.is_equal, 0.0, 0, -1), r=["ones"], w=["rep"])
-    op("pool", lambda: g.affine_select(T.id32[:, :], T.ones[:, :], [[-1, 128]], ALU.is_equal, 0.0, 0, 1), r=["ones"], w=["id32"])
-    op("pool", iota(T.kk[0:1, :], [[0, 64], [16, 4]], 0, 0, True), w=["kk0"])
+    mark(T.rep[0:8, :], "rep", [[1, 8], [0, 16]], 0, -1)
+    mark(T.idbf[:, :], "idbf", [[-1, 128]], 0, 1)
     for h in range(2):
-        own = perm[4 * h:4 * h + 4]
-        if all(own[t + 1] - own[t] == own[1] - own[0] for t in range(3)):
-            op("pool", iota(T.kk[32:33, 128 * h:128 * h + 128], [[8 * (own[1] - own[0]), 4], [1, 8], [0, 4]], 8 * own[0], 0, True),
-               r=["kk32"], w=["kk32_%d" % h])
-        else:
-            for t in range(4):
-                op("pool", iota(T.kk[32:33, 128 * h + 32 * t:128 * h + 32 * t + 32], [[1, 8], [0, 4]], 8 * own[t], 0, True),
-                   r=["kk32"], w=["kk32_%d" % h])
-    op("dve", lambda: V.tensor_copy(T.posef[0:8, 0:6], T.posei[0:8, 0:6]), r=["posei"], w=["posef"])
-    op("dve", ts(T.d16a[:, :], T.d16[:, :], 15, None, ALU.bitwise_and), r=["d16"], w=["d16a"])
-    op("pe", mms([(T.p6[:, 0:6], T.rep[0:8, :], T.posef[0:8, 0:6], True, True)]), r=["rep", "posef"], b=["p6"])
-    op("dve", lambda: V.tensor_copy(col(ICOL), T.d16a[:, 0:1]), r=["d16a"], w=["icol"])
+        op("pool", iota(T.kk[0:64, 128 * h:128 * h + 128], [[16, 4], [1, 8], [0, 4]], 8 * h, 0, True), w=["kk%d" % (2 * h), "kk%d" % (2 * h + 1)])
+    op("pool", iota(T.kx[:, :], [[0, 64], [16, 4]], 0, 0, True), w=["kx"])
+    by_height = [[-16, 8]]
+    mark(T.pm[:, :], "pm", [[-1, 16], [-16, 8]], 0, 1)
+    mark(sell, "sell0", [[-2, 2], [-16, 8]], 0, 1, 2.0 ** -12)
+    mark(T.sel[:, 17:32:2], "seld1", by_height, 0, 1)
+    op("pool", iota(T.wsc[:, 8:10], [[-128, 2]], 64, 0, True), w=["w64"])
+    op("pool", iota(T.wsc[:, 10:12], [[-62, 2]], 31, 0, True), w=["w31"])
+    mark(T.sel[:, 0:8], "sell1", by_height, -1, 1, 2.0 ** -12, T.sel[:, 0:8], after=["sell0", "seld1", "w64", "w31"])
+    mark(T.sel[:, 17:32:2], "seld2", by_height, -1, 1, 2.0 ** -9, T.sel[:, 17:32:2], after=["seld1"])
+    mark(T.sel[:, 16:32:2], "seld0", by_height, -15, 1, 16.0)
+    op("pool", iota(T.winc[:, 4224:WC], [[0, WC - 4224]], 0, 0, True), w=["wcz"])
+    mark(T.rst[:, :], "rst", [[0, 16], [1, 8]], 0, 0, test=ALU.is_equal)
+    mark(T.sel[:, 32:40], "sele0", by_height, -15, 1, -16.0)
+    mark(T.sel[:, 40:48], "sele1", by_height, -15, 1, 16.0)
+    for k, (c0, value, base, cm) in enumerate(((9, -0.125, -16, 1), (8, -0.125, -16, 1), (9, 0.125, -16, 1),
+                                               (10, 31.0 / 512, 15, -1), (11, -31.0 / 512, 15, -1))):
+        mark(T.wsc[:, k:k + 1], "wsc%d" % k, [[0, 1]], base, cm, value, T.wsc[:, c0:c0 + 1], ALU.is_ge, ["w64", "w31"])
+    op("dve", lambda: V.tensor_copy(T.poseb[0:8, 0:6], T.posei[0:8, 0:6]), r=["posei"], w=["poseh"])
+    op("dve", ts(T.ii[:, 0:1], T.d16[:, 0:1], 3, None, ALU.bitwise_and), r=["d16"], w=["ii0"])
+    op("dve", tt(T.poseb[0:8, 6:12], T.posei[0:8, 0:6], T.poseb[0:8, 0:6], ALU.subtract), r=["posei", "poseh"], w=["posel"])
+    op("dve", ts(T.ii[:, 1:2], T.d16[:, 0:1], 12, None, ALU.bitwise_and), r=["d16"], w=["ii1"])
+    op("pe", mms([(T.p6[:, 0:12], T.rep[0:8, :], T.poseb[0:8, 0:12], True, True)]), r=["rep", "poseh", "posel"], b=["p6"])
+    op("pe", mms([(T.pc1[:, 0:2], T.rep[0:8, :], T.poseb[0:8, 4:6], True, False), (T.pc1[:, 0:2], T.rep[0:8, :], T.poseb[0:8, 10:12], False, True)]),
+       r=["rep", "poseh", "posel"], b=["pc1"])
     op("dve", lambda: V.tensor_copy(T.hi[:, :], T.lensi[:, :]), r=["lensi"], w=["hi"])
-    op("act", act(col(HCOL), T.p6[:, 4:5], AF.Identity, scale=2.0 ** -12), w=["hcol"], b=["p6"])
-    op("act", act(T.ct[:, CX:CX + 33:32], T.p6[:, 0:2], AF.Copy), w=["cta"], b=["p6"])
-    op("act", act(T.ct[:, CZ:CZ + 1], T.p6[:, 1:2], AF.Identity, scale=-1.0), w=["ctb"], b=["p6"])
-    op("act", act(col(T2), T.p6[:, 3:4], AF.Identity, bias=16 - 3.5 / 8, scale=0.125), w=["t2"], b=["p6"])
-    op("act", act(col(T1), T.p6[:, 2:3], AF.Identity, bias=-15.5 / 8, scale=0.125), w=["t1"], b=["p6"])
-    op("act", act(T.ct[:, CZ + 32:CZ + 33], T.p6[:, 0:1], AF.Copy), w=["ctc"], b=["p6"])
-    op("act", act(T.ct[:, CZ + 64:CZ + 65], col(ICOL), AF.Identity, bias=col(T2), scale=T.ct[:, CZ:CZ + 1]), r=["icol", "t2", "ctb"], w=["cte"])
-    op("act", act(T.ct[:, CX + 64:CX + 65], col(ICOL), AF.Identity, bias=col(T1), scale=T.ct[:, CX:CX + 1]), r=["icol", "t1", "cta"], w=["ctd"])
-    op("act", act(col(T3), T.p6[:, 5:6], AF.Relu, bias=4095.0, scale=-1.0), w=["t3"], b=["p6"])
-    op("sync", lambda: S.dma_start(T.winl[0:128:16, 16:4112], T.hi[:, :]), r=["hi", "wl0", "wl1", "wl2", "wl3"], w=["wlhi"], tok=("dw", 48), dma=True)
-    op("dve", tt(T.lo[:, 0:128], T.lensi[:, 0:128], T.hi[:, 0:128], ALU.subtract), r=["lensi", "hi"], w=["lo0"])
-    op("dve", ts(T.vi[:, :], T.lensi[:, :], col(HCOL), 15.5 + 2.0 ** -13, ALU.mult, ALU.add), r=["lensi", "hcol"], w=["vi"])
-    op("dve", tt(T.lo[:, 128:192], T.lensi[:, 128:192], T.hi[:, 128:192], ALU.subtract), r=["lensi", "hi"], w=["lo1"])
-    op("dve", ts(T.va[:, :], T.vi[:, :], 0x7FFFFFFF, None, ALU.bitwise_and), r=["vi"], w=["va"])
-    op("dve", tt(T.lo[:, 192:256], T.lensi[:, 192:256], T.hi[:, 192:256], ALU.subtract), r=["lensi", "hi"], w=["lo2"])
-    op("sync", lambda: S.dma_start(T.winl[1:128:16, 16:4112], T.lo[:, :]), r=["lo0", "lo1", "lo2"], w=["wllo"], tok=("dw", 48), dma=True)
-    op("dve", ts(T.vt[:, :], T.va[:, :], 128.0, None, ALU.mult), r=["va"], w=["vt"])
-    op("sync", lambda: S.dma_start(T.winl[2:128:16, 16:4112], T.vt[:, :]), r=["vt"], w=["wlvt"], tok=("dw", 48), dma=True)
-    op("dve", lambda: V.memset(T.kk[64:65, :], 1.0), w=["kk64"])
-    op("dve", lambda: V.memset(T.ones2[:, :], 1.0), w=["ones2"])
-    for q in range(CUT["early"], 8):
-        cam_load(q, ["ones2"])
-    op("pool", lambda: g.affine_select(T.pm[:, :], T.ones2[:, :], [[-1, 16], [-16, 8], [1000, 2]], ALU.is_equal, 0.0, 0, 1), r=["ones2"], w=["pm"])
-    op("pool", iota(T.e16i[:, :], [[0, 16], [-1, 16]], 0, 1, False), w=["e16i"])
-    op("pool", iota(T.bndc[:, 0:2], [[-62, 2]], 31, 0, True), w=["bndc"])
-    op("pool", lambda: g.affine_select(T.bnd[:, 0:1], T.bndc[:, 0:1], [[0, 1]], ALU.is_ge, 31.0 / 512, 15, -1), r=["bndc"], w=["bnd0"])
-    op("pool", lambda: g.affine_select(T.bnd[:, 4:5], T.bndc[:, 1:2], [[0, 1]], ALU.is_ge, -31.0 / 512, 15, -1), r=["bndc"], w=["bnd1"])
-    op("pe", mms([(T.p7[0:KR, 128:256], T.ct[:, CZ:CZ + KR], T.id32[:, :], True, True),
-                  (T.p7[0:KR, 0:128], T.ct[:, CX:CX + KR], T.id32[:, :], True, True)]),
-       r=["ct", "cta", "ctb", "ctc", "ctd", "cte", "id32"], b=["p7"])
-    op("act", act(ktol, col(T3), AF.Identity, bias=4095.0 * 4096, scale=-4096.0), r=["t3"], w=["ktol"])
-    op("act", act(col(KT2), col(T3), AF.Identity, bias=4095.0 * 4096 - 128, scale=-4096.0), r=["t3"], w=["ktol2"])
-    op("act", act(T.pt[0:KR, :], T.p7[0:KR, 0:256], AF.Copy), w=["pt"], b=["p7"])
-    kkall = ["kk", "kk0", "kk32_0", "kk32_1", "kk64"]
+    op("dve", ts(T.col[:, 0:2], T.ii[:, :], -1.0, None, ALU.mult), r=["ii0", "ii1"], w=["icol"])
+    for k, (out, src, scale) in enumerate((
+            (T.ct[:, CX:CZ + 1:CZ], T.p6[:, 0:2], -1.0), (T.ct[:, CZ + 32:CZ + 33], T.p6[:, 0:1], 1.0),
+            (T.ct[:, CZ + 64:CZ + 66], T.p6[:, 3:10:6], 0.125), (T.ct[:, CX + 66:CZ + 67:CZ], T.p6[:, 0:2], T.col[:, 0:1]),
+            (T.ct[:, CX + 67:CZ + 68:CZ], T.p6[:, 0:2], T.col[:, 1:2]), (T.ct[:, CZ + 96:CZ + 98], T.p6[:, 5:12:6], -1.0),
+            (T.ct[:, CX + 32:CX + 33], T.p6[:, 1:2], -1.0), (T.ct[:, CX + 64:CX + 66], T.p6[:, 2:9:6], -0.125))):
+        op("act", act(out, src, AF.Identity, scale=scale), r=["icol"], w=[ctall[k + 1]], b=["p6"])
+    table(0, T.hi, "hi")
+    op("pe", mms([(T.pb1[:, 0:256], T.idbf[:, :], T.hi[:, :], True, True)]), r=["idbf", "hi"], b=["pb1"])
+    op("dve", ts(T.vt[:, :], T.lensi[:, :], T.pc1[:, 0:1], 4096 * 207.5 + 0.5, ALU.mult, ALU.add), r=["lensi"], w=["vt"], b=["pc1"])
+    table(2, T.vt, "vt")
+    op("dve", tt(T.lo[:, :], T.lensi[:, :], T.pb1[:, 0:256], ALU.subtract), r=["lensi"], w=["lo"], b=["pb1"])
+    table(1, T.lo, "lo")
+    op("dve", lambda: V.memset(T.kk[64:128, :], 1.0), w=["kk64"])
+    op("dve", lambda: V.tensor_copy(T.kk[0:32, :], T.kx[:, :]), r=["kx"], w=["kk0", "kk2"])
+    op("pe", mms([(T.p7[0:KR, 128:256], T.ct[:, CZ:CZ + KR], T.idbf[:, :], True, True)]), r=["ct", "idbf"] + ctall[:7], b=["p7"])
+    op("pe", mms([(T.pc0[0:KB, 0:128], T.ct[:, CX:CX + KB], T.idbf[:, :], True, True)]), r=["ct", "idbf"] + ctall, b=["pc0"])
+    op("act", act(T.pt[0:KR, 128:256], T.p7[0:KR, 128:256], AF.Copy), w=["ptz"], b=["p7"])
+    op("act", act(T.pt[0:KB, 0:128], T.pc0[0:KB, 0:128], AF.Copy), w=["ptx"], b=["pc0"])
+    kkall = ["kk0", "kk1", "kk2", "kk3", "kk64"]
+    kkof = lambda h: kkall[2 * h:2 * h + 2] + ["kk64"]
+    half = lambda t, h, r0=0, r1=KB: t[r0:r1, 128 * h:128 * h + 128]
 
     def z_base(h, stop):
-        op("pe", mms([(T["pa%d" % h][:, 0:128], T.pt[0:KR, 128:256], T.kk[0:KR, 128 * h:128 * h + 128], True, stop)]),
-           r=kkall + ["pt"], b=["pa%d" % h])
+        op("pe", mms([(T["pa%d" % h][:, 0:128], T.pt[0:KB, 128:256], half(T.kk, h), True, stop)]), r=kkof(h) + ["ptz"], b=["pa%d" % h])
 
     def x_base(h, stop):
-        op("pe", mms([(T["pb%d" % h][:, 256:384], T.kk[0:KR, 128 * h:128 * h + 128], T.pt[0:KR, 0:128], True, stop)]),
-           r=kkall + ["pt"], b=["pb%d" % h])
+        op("pe", mms([(T["pb%d" % h][:, 256:384], half(T.kk, h), T.pt[0:KB, 0:128], True, stop)]), r=kkof(h) + ["ptx"], b=["pb%d" % h])
+
+    def d_base(h):
+        pc = T["pc%d" % h]
+        op("pe", mms([(pc[:, 0:256:2], half(T.kk, h), T.pt[0:KB, 256:384], True, False),
+                      (pc[:, 1:256:2], half(T.kk, h, 0, 32), T.winc[0:32, 0:128], False, False)]), r=kkall + ["ptd", "wcy"], b=["pc%d" % h])
 
     def a_zo(p, h):
         n = "%d%d" % (p, h)
-        op("dve", ts(T["zo" + n][:, :], T["pa%d" % h][:, 0:128], 15.0, 4112.0, ALU.max, ALU.min), w=["zo" + n], b=["pa%d" % h])
+        op("dve", ts(T["zo" + n][:, :], T["pa%d" % h][:, 0:128], 16.0, 4112.0, ALU.add, ALU.min), w=["zo" + n], b=["pa%d" % h])
 
     def a_x(p, h):
         n = "%d%d" % (p, h)
-        op("dve", ts(T["xi" + n][:, :], T["pb%d" % h][:, 256:384], 0.25, None, ALU.mult), w=["xi" + n], b=["pb%d" % h])
+        op("dve", ts(T["xi" + n][:, :], T["pb%d" % h][:, 256:384], -0.25, -15.5 / 32, ALU.mult, ALU.add), w=["xi" + n], b=["pb%d" % h])
 
-    def a_nz(p, h):
-        n = "%d%d" % (p, h)
-        op("act", act(T["nz" + n][:, :], T["pa%d" % h][:, 0:128], AF.Identity, bias=-MAGIC, scale=-1.0), w=["nz" + n], b=["pa%d" % h])
-
-    wl = ["wl0", "wl1", "wl2", "wl3", "wlhi", "wllo", "wlvt"]
-    wc = ["winc%d" % q for q in range(8)] + ["wcz"]
+    wl = fill + ["wlhi", "wllo", "wlvt"]
+    wc = ["winc%d" % q for q in range(8)] + ["wcz", "wcy"]
     gall = lambda out, k0=0, k1=128: ["%s_%d" % (out, k) for k in range(k0, k1, 2)]
+
+    def tile(name, k0=0, k1=128):
+        if name[:3] in ("zo1", "xi1"):
+            return T[name[:3]][:, 128 * int(name[3]) + k0:128 * int(name[3]) + k1]
+        return T[name][:, k0:k1]
 
     def gather(e, out, off, k0, k1):
         lens = out[:2] == "gl"
         win = T.winl[:, 0:WL] if lens else T.winc[:, 0:WC]
-        src = lambda: win.indirect(T[off][:, k0:k1])
+        src = lambda: win.indirect(tile(off, k0, k1))
         dst = T[out][:, 16 * k0:16 * k1]
         if e == "dve":
             f = lambda: V.tensor_copy(dst, src())
@@ -292,84 +314,106 @@ def rank_program(g, core, T, topo):
             f = lambda: A.activation(dst, src(), AF.Copy)
         op(e, f, r=[off] + (wl if lens else wc), w=gall(out, k0, k1))
 
-    def slot(out, off, seq):
-        vtot = sum(x[1] for x in seq if isinstance(x, tuple) and x[0] == "v")
-        lo, hi = 0, 128
-        for x in seq:
-            if not isinstance(x, tuple):
-                x()
-            elif x[0] == "v":
-                gather("dve", out, off, lo, lo + x[1])
-                lo += x[1]
-            else:
-                n = hi - vtot if x[1] is None else x[1]
-                gather("act", out, off, hi - n, hi)
-                hi -= n
-        assert lo == hi
+    span = {}
 
-    def x_lens(p, h):
+    def piece(e, out, n=None):
+        key = out
+        if out[0] == "b":
+            h, t = divmod(seq[int(out[1])], 4)
+            out, off, ends = "gf%d" % h, "fo%d" % h, [32 * t, 32 * t + 32]
+        else:
+            off, ends = {"gl": "zo", "gd": "po"}[out[:2]] + out[2:], [0, 128]
+        lo, hi = span.setdefault(key, ends)
+        n = hi - lo if n is None else n
+        assert 0 <= n <= hi - lo
+        if n and e == "v":
+            gather("dve", out, off, lo, lo + n)
+            span[key][0] += n
+        elif n:
+            gather("act", out, off, hi - n, hi)
+            span[key][1] -= n
+
+    def x_lens(p, h, k0=0, k1=128):
         n = "%d%d" % (p, h)
         pb, gl = T["pb%d" % h], T["gl" + n]
-        op("pe", mms([(pb[:, i:256:16], gl[:, i:2048:16], T.sell[:, :], True, True) for i in range(16)]),
-           r=gall("gl" + n) + ["sell0", "sell1"], b=["pb%d" % h])
+        op("pe", mms([(pb[k0:k1, i:256:16], gl[:, 16 * k0 + i:16 * k1:16], sell, True, True) for i in range(16)]),
+           r=gall("gl" + n, k0, k1) + ["sell0", "sell1"], b=["pb%d" % h])
 
-    def b_steps(p, h):
+    def b_w(p, h):
         n = "%d%d" % (p, h)
-        pa, pb, pc, pen = T["pa%d" % h], T["pb%d" % h], T["pc%d" % h], T["pen" + n]
+        op("dve", tt(T["w" + n][:, :], tile("xi" + n), T["pb%d" % h][:, 0:128], ALU.mult), r=["xi" + n], w=["w" + n], b=["pb%d" % h])
 
-        def b1():
-            op("dve", tt(T["w" + n][:, :], T["xi" + n][:, :], pb[:, 0:128], ALU.mult), r=["xi" + n], w=["w" + n], b=["pb%d" % h])
-            op("act", act(T["vb" + n][:, :], pb[:, 128:256], AF.Copy), w=["vb" + n], b=["pb%d" % h])
-            op("act", act(T["q" + n][:, :], T["w" + n][:, :], AF.Abs, bias=0.5, scale=4096.0), r=["w" + n], w=["q" + n])
+    def b_v(p, h):
+        n = "%d%d" % (p, h)
+        op("act", act(T["vb" + n][:, :], T["pb%d" % h][:, 128:256], AF.Identity, scale=128.0), w=["vb" + n], b=["pb%d" % h])
 
-        def b2():
-            op("dve", ts(T["ub" + n][:, :], T["w" + n][:, :], 191.5 + 2.0 ** -13, 128.0, ALU.add, ALU.max), r=["w" + n], w=["ub" + n])
-            op("pe", mms([(pa[:, 128:256], T["ub" + n][:, :], T.idbf[:, :], True, False),
-                          (pa[:, 128:256], T["vb" + n][:, :], T.idbf[:, :], False, True)]), r=["vb" + n, "ub" + n, "idbf"], b=["pa%d" % h])
+    def b_q(p, h):
+        n = "%d%d" % (p, h)
+        op("act", act(T["q" + n][:, :], T["w" + n][:, :], AF.Abs, bias=0.5, scale=4096.0), r=["w" + n], w=["q" + n])
 
-        def b3():
-            op("dve", ts(T["po" + n][:, :], pa[:, 128:256], 128.0, 4096.0, ALU.subtract, ALU.min), w=["po" + n], b=["pa%d" % h])
+    def pixel(p, h, c0, stop):
+        n = "%d%d" % (p, h)
+        out = T["pa%d" % h][:, c0:c0 + 128]
+        op("pe", mms([(out, T["ub" + n][:, :], T.idbf[:, :], True, False), (out, T["vb" + n][:, :], T.idbf[:, :], False, stop)]),
+           r=["vb" + n, "ub" + n, "idbf"], b=["pa%d" % h])
 
-        def b4():
-            op("act", act(pen[:, :], T["q" + n][:, :], AF.Relu, bias=-(2.0 ** 35), scale=2.0 ** 17), r=["q" + n], w=["pen" + n])
-            if p == 1:
-                op("pe", mms([(pc[:, 2 * x:256:16], T.idbf[:, :], pen[:, 16 * x:16 * x + 16], False, False) for x in range(8)]),
-                   r=["pen" + n, "idbf"], b=["pc%d" % h])
-            else:
-                a_nz(p, h)
-                op("act", act(T["sn%d" % h][:, :], pa[:, 128:256], AF.Identity, bias=col(KT2)), r=["ktol2"], w=["sn%d" % h], b=["pa%d" % h])
-                op("pe", mms([(pc[:, 0:128], T["nz" + n][:, :], T.id32[:, :], True, False), (pc[:, 0:128], T.idbf[:, :], pen[:, :], False, False)]),
-                   r=["pen" + n, "idbf", "id32", "nz" + n], b=["pc%d" % h])
-        c = CUT["b"]
-        return [("v", c[0]), ("a", CUT["ba"]), b1, ("a", None), ("v", c[1]), b2, ("v", c[2]), b3, ("v", c[3])], b4
+    def b_u(p, h):
+        n = "%d%d" % (p, h)
+        op("dve", ts(T["ub" + n][:, :], T["w" + n][:, :], 191.5 + 2.0 ** -13, 128.0, ALU.add, ALU.max), r=["w" + n], w=["ub" + n])
 
-    def x_depth(p, h):
+    def b_off(p, h):
+        n = "%d%d" % (p, h)
+        op("dve", ts(T["po" + n][:, :], T["pa%d" % h][:, 128:256], POFF, 4224.0, ALU.subtract, ALU.min), w=["po" + n], b=["pa%d" % h])
+
+    def b_pen(p, h):
+        n = "%d%d" % (p, h)
+        pc, pen = T["pc%d" % h], T["pen" + n]
+        op("act", act(pen[:, :], T["q" + n][:, :], AF.Relu, bias=-(2.0 ** 35), scale=2.0 ** 17), r=["q" + n], w=["pen" + n])
+        if p == 1:
+            op("pe", mms([(pc[:, 2 * x:256:16], T.idbf[:, :], pen[:, 16 * x:16 * x + 16], False, False) for x in range(8)]),
+               r=["pen" + n, "idbf"], b=["pc%d" % h])
+        else:
+            op("pe", mms([(pc[:, 0:128], T.idbf[:, :], pen[:, :], False, False)]), r=["pen" + n, "idbf"], b=["pc%d" % h])
+            pixel(p, h, 256, False)
+
+    def x_depth(p, h, k0=0, k1=128):
         n = "%d%d" % (p, h)
         pc, gd = T["pc%d" % h], T["gd" + n]
-        if p == 1:
-            lst = [(pc[:, 16 * i:16 * i + 16], gd[:, i:2048:16], T.seld[:, :], False, i == 15) for i in range(16)]
-        else:
-            lst = [(pc[:, i:128:16], gd[:, i:2048:16], T.seld[:, 0:16:2], False, i == 15) for i in range(16)]
-        op("pe", mms(lst), r=gall("gd" + n) + ["seld0", "seld1"], b=["pc%d" % h])
+        last = k0 <= 32 < k1
+        lst = [(pc[k0:k1, 16 * i:16 * i + 16] if p == 1 else pc[k0:k1, i:256:16], gd[:, 16 * k0 + i:16 * k1:16],
+                seld if p == 1 else sele, False, last and i == 15) for i in range(16)]
+        op("pe", mms(lst), r=gall("gd" + n, k0, k1) + (["seld0", "seld2"] if p == 1 else ["sele0", "sele1"]), b=["pc%d" % h])
 
-    def c_abs(p, h):
-        pa, pc = T["pa%d" % h], T["pc%d" % h]
-        if p == 1:
-            op("act", act(pc[:, 256:384], pc[:, 0:256:2], AF.Abs, bias=4096.0 * (MAGIC + 16), scale=4096.0), b=["pc%d" % h])
-        else:
-            op("act", act(T["ab%d" % h][:, :], pc[:, 0:128], AF.Abs, bias=4096.0 * (MAGIC + 16), scale=4096.0), w=["ab%d" % h], b=["pc%d" % h])
-            op("pe", mms([(pa[:, 256:384], T["ab%d" % h][:, :], T.id32[:, :], True, True)]), r=["ab%d" % h, "id32"], b=["pa%d" % h])
+    def c_abs(h):
+        op("act", act(T["ab%d" % h][:, :], T["pc%d" % h][:, 0:256:2], AF.Abs), w=["ab%d" % h], b=["pc%d" % h])
 
     def c_sums(h):
         pc, sc, snd = T["pc%d" % h], T["sc%d" % h], T["snd%d" % h]
         mk, mv = T["mk%d" % h], T["mv%d" % h]
         return [
-            lambda: op("dve", tt(mk[:, :], pc[:, 256:384], T.tolt[:, :], ALU.is_le), r=["tolt"], w=["mk%d" % h], b=["pc%d" % h]),
+            lambda: op("dve", tt(mk[:, :], T["ab%d" % h][:, :], T.p6[:, 128:256], ALU.is_le), r=["ab%d" % h], w=["mk%d" % h], b=["p6"]),
             lambda: op("dve", tt(mv[:, :], mk[:, :], pc[:, 1:256:2], ALU.mult), r=["mk%d" % h], w=["mv%d" % h], b=["pc%d" % h]),
             lambda: op("dve", lambda: V.tensor_tensor_scan(sc[:, :], T.rst[:, :], mv[:, :], 0.0, ALU.mult, ALU.add),
                        r=["mv%d" % h, "rst"], w=["sc%d" % h]),
             lambda: op("dve", ts(snd[:, 0:16], sc[:, 7:128:8], MAGIC, MAGIC, ALU.add, ALU.subtract), r=["sc%d" % h], w=["sna%d" % h]),
             lambda: op("dve", tt(snd[:, 16:32], sc[:, 7:128:8], snd[:, 0:16], ALU.subtract), r=["sc%d" % h, "sna%d" % h], w=["snb%d" % h])]
+
+    def ab_base(h):
+        pc = T["pc%d" % h]
+        op("pe", mms([(pc[:, 0:256], T["sh%d" % h][:, :], T.ww[:, 128:384], True, False),
+                      (pc[:, 0:128], half(T.kk, h, 0, KR), T.pt[0:KR, 128:256], False, False),
+                      (pc[:, 128:256], half(T.kn, h), T.pt[0:KB, 128:256], False, False)]),
+           r=kkall + ["kn", "ptz", "ww1", "ww2", "sh%d" % h], w=["test%d" % h], b=["pc%d" % h])
+        op("pe", mms([(pc[:, 128:256], half(T.kk, h, 96, KR), T.pt[96:KR, 128:256], False, False)]), r=["test%d" % h], b=["pc%d" % h])
+
+    def c_fail(h):
+        pa, gb = T["pa%d" % h], T["gb%d" % h]
+        op("act", act(gb[:, :], T["pc%d" % h][:, 0:256], AF.Relu, scale=2.0 ** 24), w=["gb%d" % h], b=["pc%d" % h])
+        op("pe", mms([(pa[:, 256:384], gb[:, 128 * x:128 * x + 128], T.idbf[:, :], False, x == 1) for x in range(2)]),
+           r=["gb%d" % h, "idbf"], b=["pa%d" % h])
+
+    def c_off(h):
+        op("dve", ts(T["fo%d" % h][:, :], T["pa%d" % h][:, 256:384], POFF, 4224.0, ALU.subtract, ALU.min), w=["fo%d" % h], b=["pa%d" % h])
 
     left = [0]
 
@@ -379,35 +423,54 @@ def rank_program(g, core, T, topo):
 
     def send_shift(h):
         snd, land = T["snd%d" % h][:, :], T["rcv%d" % h][:, rank, :]
-        sem = T.sem["xa%d" % h]
 
-        def f():
-            tr = [RemoteDMATransfer(dst_ids=[dst_id(r) for r in grp], dma_engine_mask=m, remote_sem=sem,
-                                    srcs=[snd], dsts=[land for _r in grp]) for grp, m in ((far, moff), (near, mon[h]))]
-            return g.remote_dma_fused(tr, local_sem=T.sem.ls)
+        def call(sem, *parts):
+            tr = [RemoteDMATransfer(dst_ids=[dst_id(r) for r in grp], dma_engine_mask=m, remote_sem=T.sem[sem],
+                                    srcs=[snd], dsts=[land for _r in grp]) for grp, m in parts]
+            op("pool", lambda: g.remote_dma_fused(tr, local_sem=T.sem.ls), r=["sna%d" % h, "snb%d" % h], tok=("ls", 0))
+        second = [r for r in far if second_call(rank, r)]
+        call("xa%d" % h, ([r for r in far if r not in second], moff), (near, mon[h]))
         left[0] += noff + HOME[h]
-        op("pool", f, r=["sna%d" % h, "snb%d" % h], tok=("ls", 0))
+        if second:
+            call("xb%d" % h, (second, moff))
+            left[0] += noff
+
+    sbank = ("p7", "p6")
 
     def shift_own(h):
-        op("pe", mms([(T["pc%d" % h][0:32, 384:512], T["snd%d" % h][:, :], T.idbf[:, :], True, False)]),
-           r=["sna%d" % h, "snb%d" % h, "idbf"], b=["pc%d" % h])
+        op("pe", mms([(T[sbank[h]][0:32, 384:512], T["snd%d" % h][:, :], T.idbf[:, :], True, False)]),
+           r=["sna%d" % h, "snb%d" % h, "idbf"], b=[sbank[h]])
 
     def shift_sum(h):
-        pa, pb, pc, sh = T["pa%d" % h], T["pb%d" % h], T["pc%d" % h], T["sh%d" % h]
-        op("ext", None, w=["rcv%d" % h], tok=("xa%d" % h, sum(incs(r, h) for r in others)))
-        op("pe", mms([(pc[0:32, 384:512], T["rcv%d" % h][:, r, :], T.idbf[:, :], False, r == others[-1]) for r in others]),
-           r=["rcv%d" % h], b=["pc%d" % h])
-        op("dve", ts(sh[:, :], pc[0:32, 384:512], T.bnd[:, 4:5], T.bnd[:, 0:1], ALU.max, ALU.min), r=["bnd0", "bnd1"], w=["sh%d" % h], b=["pc%d" % h])
-        op("pe", mms([(pa[:, 0:128], T.ww[:, 128:256], sh[:, :], False, True)]), r=["ww", "sh%d" % h], b=["pa%d" % h])
-        op("pe", mms([(pb[:, 256:384], sh[:, :], T.ww[:, 0:128], False, True)]), r=["ww", "sh%d" % h], b=["pb%d" % h])
+        second = [r for r in others if second_call(r, rank)]
+        groups = [(s, grp) for s, grp in (("xa%d" % h, [r for r in others if r not in second]), ("xb%d" % h, second)) if grp]
+        for s, grp in groups:
+            op("ext", None, w=[s], tok=(s, sum(incs(r, h) for r in grp)))
+            op("pe", mms([(T[sbank[h]][0:32, 384:512], T["rcv%d" % h][:, r, :], T.idbf[:, :], False, r == groups[-1][1][-1]) for r in grp]),
+               r=[s], b=[sbank[h]])
 
-    def c_keep(h):
-        op("dve", tt(T["kp%d" % h][:, :], T["sn%d" % h][:, :], T["pa%d" % h][:, 256:384], ALU.max), r=["sn%d" % h], w=["kp%d" % h], b=["pa%d" % h])
+    def shift_clamp(h):
+        pa, pb, sh = T["pa%d" % h], T["pb%d" % h], T["sh%d" % h]
+        op("dve", ts(sh[:, :], T[sbank[h]][0:32, 384:512], T.wsc[:, 4:5], T.wsc[:, 3:4], ALU.max, ALU.min),
+           r=["wsc3", "wsc4"], w=["sh%d" % h], b=[sbank[h]])
+        op("pe", mms([(pa[:, 0:128], T.ww[:, 128:256], sh[:, :], False, True)]), r=["ww1", "sh%d" % h], b=["pa%d" % h])
+        op("pe", mms([(pb[:, 256:384], sh[:, :], T.ww[:, 0:128], False, True)]), r=["ww0", "sh%d" % h], b=["pb%d" % h])
 
-    def c_off(h):
-        op("dve", ts(T["fo%d" % h][:, :], T["kp%d" % h][:, :], ktol, 4096.0, ALU.subtract, ALU.min), r=["ktol", "kp%d" % h], w=["fo%d" % h])
+    def shift_weights():
+        for k in range(3):
+            op("act", act(T.wt[:, 16 * k:16 * k + 16], T.selc[:, :], AF.Identity, scale=T.col[:, 4 + k % 2:5 + k % 2]),
+               r=["selc", "abf"], w=["wt%d" % k])
 
-    fbank = lambda j: (("pb0", "pc0", "pb1")[j % 3], 64 * (j // 3))
+    def turn_weights():
+        op("pe", mms([(T.p7[0:32, 128 * k:128 * k + 128], T.wt[:, 16 * k:16 * k + 32], T.idbf[:, :], True, True) for k in range(2)]),
+           r=["wt0", "wt1", "wt2", "idbf"], b=["p7"])
+
+    def keep_weights():
+        for k, c0 in ((1, 128), (0, 0), (2, 128)):
+            op("act", act(T.ww[:, 128 * k:128 * k + 128], T.p7[0:32, c0:c0 + 128], AF.Identity, scale=T.wsc[:, k:k + 1]),
+               r=["wsc%d" % k], w=["ww%d" % k], b=["p7"])
+
+    fbank = lambda j: (("pb0", "pc0", "pa0")[j % 3], 64 * (j // 3))
 
     def f_sum(b, j):
         h, t = divmod(b, 4)
@@ -422,118 +485,64 @@ def rank_program(g, core, T, topo):
         src = T.fout[:, b, :]
         op("dve", lambda: V.tensor_copy(src, T[bk][:, c0:c0 + 64]), w=["fout%d" % b], b=[bk])
         if owner != rank:
-            m = moff if owner in far else mon[2]
             rid, pid, _se = topo.addr(cores[owner])
-            left[0] += noff if owner in far else HOME[2]
+            left[0] += noff
             sem = T.sem["fb" if is_late(rank, owner) else "fa"]
-            op("pool", lambda: g.remote_dma(T.frecv[:, rank, :], src, sem, T.sem.ls, pid, rid, m), r=["fout%d" % b], tok=("ls", 0))
+            op("pool", lambda: g.remote_dma(T.frecv[:, rank, :], src, sem, T.sem.ls, pid, rid, moff), r=["fout%d" % b], tok=("ls", 0))
 
-    z_base(0, True)
-    z_base(1, True)
-    x_base(0, True)
-    x_base(1, True)
-    op("dve", tt(T.selt[:, 8:16], T.id32[:, 0:128:16], T.id32[:, 1:128:16], ALU.add), r=["id32"], w=["selu"])
-    op("dve", lambda: V.tensor_copy(T.sell[:, 8:16], T.id32[:, 2:128:16]), r=["id32"], w=["sell1"])
-    op("dve", lambda: V.memset(T.winc[:, 4096:WC], 0.0), w=["wcz"])
-    op("dve", lambda: V.memset(T.rst[:, :], 1.0), w=["rst"])
-    op("dve", ts(T.sell[:, 0:8], T.selt[:, 8:16], 2.0 ** -12, None, ALU.mult), r=["selu"], w=["sell0"])
-    op("act", act(T.selt[:, 0:8], T.id32[:, 1:128:16], AF.Identity, scale=2.0 ** -9), r=["id32"], w=["selt"])
-    op("act", act(T.idbf[:, :], T.id32[:, :], AF.Copy), r=["id32"], w=["idbf"])
-    op("act", act(T.seld[:, 0:16:2], T.id32[:, 15:128:16], AF.Identity, scale=16.0), r=["id32"], w=["seld0"])
-    op("act", act(T.kb[:, :], T.ones[:, :], AF.Identity, scale=ktol), r=["ones", "ktol"], w=["kb"])
-    a_zo(1, 0)
-    op("dve", tt(T.seld[:, 1:16:2], T.id32[:, 0:128:16], T.selt[:, 0:8], ALU.add), r=["id32", "selt"], w=["seld1"])
-    op("dve", lambda: V.memset(T.rst[:, 0:128:8], 0.0), w=["rst"])
-    a_zo(1, 1)
-    a_nz(1, 0)
-    a_nz(1, 1)
-    a_x(1, 0)
-    a_x(1, 1)
-    op("pe", mms([(T.p6[:, 128:256], T.kb[:, :], T.pm[:, 0:256:2], True, True)]), r=["kb", "pm"], b=["p6"])
-    for h in range(2):
-        op("pe", mms([(T["pc%d" % h][:, 0:256], T["nz1%d" % h][:, :], T.pm[:, :], True, False)]), r=["nz1%d" % h, "pm"], b=["pc%d" % h])
+    op("pe", mms([(T.pa0[:, 0:256], T.pt[0:KB, 128:256], T.kk[0:KB, :], True, True)]), r=kkall + ["ptz"], b=["pa0"])
+    op("pe", mms([(T.pb0[:, 256 + 128 * h:384 + 128 * h], half(T.kk, h), T.pt[0:KB, 0:128], True, True) for h in range(2)]),
+       r=kkall + ["ptx"], b=["pb0"])
+    op("dve", ts(T.zo1[:, :], T.pa0[:, 0:256], 16.0, 4112.0, ALU.add, ALU.min), w=["zo10", "zo11"], b=["pa0"])
+    for q in range(CUT["early"], 8):
+        cam_load(q, [CUT["gate"]])
+    op("dve", ts(T.xi1[:, :], T.pb0[:, 256:512], -0.25, -15.5 / 32, ALU.mult, ALU.add), w=["xi10", "xi11"], b=["pb0"])
+    op("pe", mms([(T.p7[0:KR, 256:384], T.ct[:, CZ:CZ + KR], T.pm[:, :], True, True)]), r=["ct", "pm"] + ctall, b=["p7"])
 
-    slot("gl10", "zo10", [("v", CUT["plain"]), ("a", None)])
-    x_lens(1, 0)
-    seq, b4 = b_steps(1, 0)
-    slot("gl11", "zo11", seq)
-    x_lens(1, 1)
-    b4()
-    seq, b4 = b_steps(1, 1)
-    slot("gd10", "po10", seq)
-    x_depth(1, 0)
-    op("act", act(T.tolt[:, :], T.p6[:, 128:256], AF.Copy), w=["tolt"], b=["p6"])
-    c = CUT["c1"]
-    seq = [("v", c[0]), ("a", CUT["c1a"]), lambda: c_abs(1, 0), b4, ("a", None)]
-    steps = c_sums(0)
-    for st in steps[:-1]:
-        seq += [st, ("v", c[1])] if c[1] else [st]
-    slot("gd11", "po11", seq + [steps[-1], lambda: send_shift(0), ("v", c[2])])
-    x_depth(1, 1)
-    c_abs(1, 1)
-    op("dve", lambda: V.memset(T.selw[:, :], 0.0), w=["selw"])
-    op("dve", ts(T.e16a[:, :], T.e16i[:, :], 15, None, ALU.bitwise_and), r=["e16i"], w=["e16a"])
-    op("dve", ts(T.selc[:, :], T.d16a[:, :], 0.0, None, ALU.is_equal), r=["d16a"], w=["selc"])
-    op("dve", lambda: V.memset(T.selw[0:1, 0:16], 0.125), r=["selw"], w=["selw0"])
-    op("dve", lambda: V.memset(T.selw[32:33, 16:32], 64.0), r=["selw"], w=["selw1"])
-    for st in c_sums(1):
-        st()
-    send_shift(1)
-    op("dve", ts(T.e16[:, :], T.e16a[:, :], 0.0, None, ALU.is_equal), r=["e16a"], w=["e16"])
-    op("pe", mms([(T.p7[0:32, 256:512], T.selw[0:KR, :], T.pt[0:KR, :], True, True)]), r=["selw", "selw0", "selw1", "pt"], b=["p7"])
-    for h in range(2):
-        z_base(h, False)
-        x_base(h, False)
-        shift_own(h)
-    op("dve", tt(T.ww[:, :], T.e16[:, :], T.p7[0:32, 256:512], ALU.mult), r=["e16"], w=["ww"], b=["p7"])
-    op("dve", lambda: V.tensor_copy(T.id16[:, :], T.id32[:, :]), r=["id32"], w=["id16"])
-
-    shift_sum(0)
-    a_zo(2, 0)
-    c = CUT["x"]
-    slot("gl20", "zo20", [("a", None), lambda: a_x(2, 0), ("v", c[0]), lambda: shift_sum(1), ("v", c[1]),
-                          lambda: a_zo(2, 1), lambda: a_x(2, 1)])
-    x_lens(2, 0)
-    seq, b4 = b_steps(2, 0)
-    slot("gl21", "zo21", seq)
-    x_lens(2, 1)
-    b4()
-    seq, b4 = b_steps(2, 1)
-    slot("gd20", "po20", seq)
-    x_depth(2, 0)
-    c = CUT["c2"]
-    slot("gd21", "po21", [("v", c[0]), ("a", CUT["c2a"]), lambda: c_abs(2, 0), b4, ("a", None), lambda: c_keep(0),
-                          ("v", c[1]), lambda: c_off(0), ("v", c[2])])
-    x_depth(2, 1)
-    seq = _blocks(topo, cores, perm, rank)
-    for j, b in enumerate(seq):
-        h, t = divmod(b, 4)
-        gf, fo, k0, kv = "gf%d" % h, "fo%d" % h, 32 * t, CUT["f"][j]
-        gather("act", gf, fo, k0 + kv, k0 + 32)
-        if j >= 6:
-            gather("dve", gf, fo, k0, k0 + 6)
-            f_out(seq[j - 1], j - 1)
-            gather("dve", gf, fo, k0 + 6, k0 + kv)
+    def more(k):
+        if k == 0:
+            op("dve", ts(T.d16a[:, :], T.d16[:, :], 15, None, ALU.bitwise_and), r=["d16"], w=["d16a"])
+            op("dve", ts(T.selc[:, :], T.d16a[:, :], 0.0, None, ALU.is_equal), r=["d16a"], w=["selc"])
+        elif k == 1:
+            op("dve", lambda: V.tensor_copy(T.id16[:, :], T.idbf[:, :]), r=["idbf"], w=["id16"])
+        elif k == 2:
+            op("act", act(T.col[:, 4:6], T.p6[:, 0:2], AF.Copy), w=["abf"], b=["p6"])
+        elif k == 3:
+            op("dve", ts(T.kn[0:KB, :], T.kk[0:KB, :], -1.0, None, ALU.mult), r=kkall, w=["kn"])
         else:
-            gather("dve", gf, fo, k0, k0 + kv)
-        if j == 2:
-            c_keep(1)
-        if 0 < j < 6:
-            f_out(seq[j - 1], j - 1)
-        if j == 2:
-            c_off(1)
-        f_sum(b, j)
-        if j == 0:
-            c_abs(2, 1)
-    f_out(seq[7], 7)
+            op("act", act(T.pt[0:KR, 256:384], T.p7[0:KR, 256:384], AF.Identity, scale=-1.0), w=["ptd"], b=["p7"])
+            d_base(0)
+            d_base(1)
+            op("pe", mms([(T.p6[:, 128:256], half(T.kk, 0, 96, KR), T.pt[96:KR, 256:384], True, True)]), r=["kk64", "ptd"], b=["p6"])
+
+    seq = _blocks(topo, cores, perm, rank)
+    sums = [c_sums(0), c_sums(1)]
+    by_pass = {"lens": x_lens, "w": b_w, "row": b_v, "q": b_q, "u": b_u, "turn": lambda p, h: pixel(p, h, 128, True),
+               "off": b_off, "pen": b_pen, "depth": x_depth, "z": a_zo, "x": a_x}
+    by_half = {"abs": c_abs, "sum": lambda h: sums[h].pop(0)(), "send": send_shift, "own": shift_own, "add": shift_sum, "clamp": shift_clamp,
+               "base": lambda h: (z_base(h, False), x_base(h, False)), "test": ab_base, "fail": c_fail, "last": c_off,
+               "weights": lambda k: (shift_weights, turn_weights, keep_weights)[k](), "more": more,
+               "fold": lambda j: f_sum(seq[j], j), "out": lambda j: f_out(seq[j], j)}
+    for step in PLAN.split():
+        if step[1] == ":":
+            e, out, n = (step.split(":") + [None])[:3]
+            piece(e, out, n and int(n))
+        elif ":" in step:
+            name, k0, k1 = step.split(":")
+            by_pass[name[:-2]](int(name[-2]), int(name[-1]), int(k0), int(k1))
+        elif step[:-2] in by_pass:
+            by_pass[step[:-2]](int(step[-2]), int(step[-1]))
+        else:
+            by_half[step[:-1]](int(step[-1]))
+    assert all(lo == hi for lo, hi in span.values())
     op("pe", mms([(T.p6[0:64, 256:384], T.fout[:, seq[7], :], T.id16[:, :], True, False)]), r=["fout%d" % seq[7], "id16"], b=["p6"])
     groups = [(s, grp) for s, grp in (("fa", early), ("fb", late)) if grp]
     for s, grp in groups:
         op("ext", None, w=[s], tok=(s, sum(incs(r, 2) for r in grp)))
         op("pe", mms([(T.p6[0:64, 256:384], T.frecv[:, r, :], T.id16[:, :], False, s == groups[-1][0] and r == grp[-1]) for r in grp]),
            r=[s], b=["p6"])
-    op("dve", lambda: V.tensor_copy(T.yb[:, :], T.p6[0:64, 256:384]), w=["yb"], b=["p6"])
-    op("sync", lambda: S.dma_start(T.y[:], T.yb[:, :]), r=["yb"], tok=("dy", 16), dma=True)
+    op("act", act(T.yb[:, :], T.p6[0:64, 256:384], AF.Copy), w=["yb"], b=["p6"])
+    op("act", lambda: A.dma_start(T.y[:], T.yb[:, :]), r=["yb"], tok=("dy", 16), dma=True)
     _emit(g, T, ops)
     g.wait_ge(T.sem.ls, left[0])
-    S.wait_ge(T.sem.dy, 16)
+    A.wait_ge(T.sem.dy, 16)

from concourse.bass import DstId, RemoteDMATransfer
from concourse.mybir import AluOpType as ALU, ActivationFunctionType as AF

N = 8
F32, BF, I32, U16, F16 = "float32", "bfloat16", "int32", "uint16", "float16"
MAGIC = 12582912.0
POFF = 128.0 * 192
WL, WC = 4128, 4240

SCRATCH = {
    "lensi": ("sbuf", [128, 256], I32), "posei": ("sbuf", [8, 8], I32), "poseb": ("sbuf", [8, 16], BF),
    "zo1": ("sbuf", [128, 256], U16), "xi1": ("sbuf", [128, 256], I32),
    "hi": ("sbuf", [128, 256], BF), "lo": ("sbuf", [128, 256], BF), "vt": ("sbuf", [128, 256], BF),
    "winl": ("sbuf", [128, WL], BF), "winc": ("sbuf", [128, WC], BF),
    "rep": ("sbuf", [8, 128], BF), "pm": ("sbuf", [128, 128], BF), "rst": ("sbuf", [128, 128], BF),
    "idbf": ("sbuf", [128, 128], BF), "id16": ("sbuf", [128, 128], F16),
    "d16": ("sbuf", [128, 16], I32), "d16a": ("sbuf", [128, 16], I32), "ii": ("sbuf", [128, 2], I32),
    "wsc": ("sbuf", [32, 12], F32), "wt": ("sbuf", [128, 48], BF),
    "sel": ("sbuf", [128, 48], BF), "selc": ("sbuf", [128, 16], BF),
    "col": ("sbuf", [128, 8], F32), "ct": ("sbuf", [128, 176], BF), "pt": ("sbuf", [128, 384], BF),
    "kk": ("sbuf", [128, 256], BF), "kn": ("sbuf", [128, 256], BF), "kx": ("sbuf", [32, 256], BF), "ww": ("sbuf", [32, 384], BF),
    "frecv": ("sbuf", [128, N, 64], F16), "fout": ("sbuf", [128, N, 64], F16), "yb": ("sbuf", [64, 128], F32),
}
for _h in range(2):
    for _n in ("ab", "mk", "mv", "sc"):
        SCRATCH["%s%d" % (_n, _h)] = ("sbuf", [128, 128], F32)
    SCRATCH["gb%d" % _h] = ("sbuf", [128, 256], BF)
    SCRATCH["snd%d" % _h] = ("sbuf", [128, 32], BF)
    SCRATCH["rcv%d" % _h] = ("sbuf", [128, N, 32], BF)
    SCRATCH["sh%d" % _h] = ("sbuf", [32, 128], BF)
    SCRATCH["fo%d" % _h] = ("sbuf", [128, 128], U16)
    SCRATCH["gf%d" % _h] = ("sbuf", [128, 2048], BF)
    for _p in (1, 2):
        for _n, _d in (("zo", U16), ("po", U16), ("xi", I32), ("ub", BF), ("vb", BF), ("w", F32), ("q", F32), ("pen", BF)):
            SCRATCH["%s%d%d" % (_n, _p, _h)] = ("sbuf", [128, 128], _d)
        SCRATCH["gl%d%d" % (_p, _h)] = ("sbuf", [128, 2048], BF)
        SCRATCH["gd%d%d" % (_p, _h)] = ("sbuf", [128, 2048], BF)
    for _b in "abc":
        SCRATCH["p%s%d" % (_b, _h)] = ("psum", [128, 512], F32)
SCRATCH["p6"] = ("psum", [128, 512], F32)
SCRATCH["p7"] = ("psum", [128, 512], F32)

SEMAPHORES = ["pe", "dve", "act", "pool", "dl", "dp", "dw", "dc", "dy", "xa0", "xa1", "xb0", "xb1", "fa", "fb", "ls"]

CUT = {"first": 4, "fill": (640, 640, 640, 512), "gate": "zo10", "early": 2, "late": 5}
PLAN = """
more4 v:gl10:58 a:gl10 lens10
v:gl11:48 a:gl11:54 w10 row10 q10 u10 turn10 v:gl11:16 a:gl11 off10 lens11 pen10
v:gd10:32 a:gd10:40 w11 row11 u11 turn11 a:gd10:26 v:gd10 depth10 off11 q11 pen11
v:gd11:28 a:gd11:8 abs0 a:gd11:66 sum0 sum0 sum0 sum0 sum0 send0 v:gd11 more0 base0 depth11 more2 weights0 abs1 weights1 more1 weights2
sum1 sum1 sum1 sum1 sum1 send1 more3 base1 own0
add0 clamp0 z20 a:gl20:74 x20 own1 test0 add1 v:gl20:48 clamp1 v:gl20 z21 lens20
v:gl21:36 a:gl21:56 w20 x21 row20 q20 a:gl21:14 test1 u20 turn20 v:gl21:20 off20 v:gl21 lens21 pen20
v:gd20:40 a:gd20:50 w21 row21 a:gd20:18 q21 u21 turn21 v:gd20:20 off21 v:gd20 depth20
v:gd21:50 a:gd21:44 fail0 pen21 a:gd21:10 v:gd21 last0 depth21
a:b0:18 v:b0 a:b1:6 fold0 fail1 v:b1 out0 fold1 a:b2:24 v:b2 last1 out1 fold2
a:b3:8 v:b3 out2 fold3 a:b4:22 v:b4 out3 fold4 a:b5:18 v:b5 out4 fold5
a:b6:22 v:b6:10 out5 v:b6 fold6 a:b7:18 v:b7:4 out6 v:b7 fold7 out7
"""
HOME = (2, 2)


def _masks(topo, cores, src):
    off = [set(topo.engines(src, c)) for c in cores if topo.chip(c) != topo.chip(src)]
    on = [topo.engines(src, c) for c in cores if c != src and topo.chip(c) == topo.chip(src)]
    far = sorted(set.intersection(*off))
    rest = [e for e in on[0] if e not in far]
    return sum(1 << e for e in far), len(far), rest[0::2] + rest[1::2]


def _blocks(topo, cores, perm, rank):
    chip = lambda b: topo.chip(cores[perm[b]])
    mine = perm.index(rank)
    seq = []
    for h in range(2):
        seq += [b for b in (4 * h + (mine + d) % 4 for d in (1, 2, 3, 4)) if chip(b) != chip(mine)]
    return seq + [b for b in range(N) if b not in seq and b != mine] + [mine]


def _emit(g, T, ops):
    queue = {"pe": g.tensor, "dve": g.vector, "act": g.scalar, "pool": g, "sync": g.sync}
    counted = ("pe", "dve", "act", "pool")
    last_w, readers, bank = {}, {}, {}
    known = {e: {} for e in queue}
    place = {e: 0 for e in counted}
    for o in ops:
        deps = []
        for r in o["r"]:
            assert r in last_w, r
            deps.append(last_w[r])
        for w in o["w"]:
            if w in last_w:
                deps.append(last_w[w])
            deps.extend(readers.get(w, []))
        for b in o["b"]:
            if b in bank and bank[b]["e"] != o["e"]:
                deps.append(bank[b])
        if o["tok"] is None and o["e"] in counted:
            place[o["e"]] += 1
            o["key"] = (o["e"], place[o["e"]])
        else:
            o["key"] = o["tok"]
        o["waits"] = []
        if o["e"] in queue:
            k = known[o["e"]]
            for d in sorted(deps, key=lambda d: -d["n"]):
                s, v = d["key"]
                if k.get(s, 0) < v:
                    o["waits"].append(d)
                    d["used"] = True
                    k[s] = v
                    for s2, v2 in d["seen"].items():
                        if k.get(s2, 0) < v2:
                            k[s2] = v2
            o["seen"] = dict(k)
        else:
            o["seen"] = {}
        for r in o["r"]:
            readers.setdefault(r, []).append(o)
        for w in o["w"]:
            last_w[w] = o
            readers[w] = []
        for b in o["b"]:
            bank[b] = o
    total = {e: 0 for e in counted}
    for o in ops:
        if o["tok"] is None and o["used"]:
            total[o["e"]] += 1
            o["val"] = total[o["e"]]
        elif o["tok"] is not None:
            o["val"] = o["tok"][1]
    for o in ops:
        if o["e"] not in queue:
            continue
        for d in o["waits"]:
            queue[o["e"]].wait_ge(T.sem[d["key"][0]], d["val"])
        ins = o["f"]()
        if o["tok"] is None and o["used"]:
            ins.then_inc(T.sem[o["e"]], 1)
        elif o["dma"]:
            ins.then_inc(T.sem[o["tok"][0]], 16)


def rank_program(g, core, T, topo):
    rank = T.rank_of(core)
    if rank is None:
        return
    cores = list(T.cores)
    perm = list(range(0, N, 2)) + list(range(1, N, 2))
    moff, noff, rest = _masks(topo, cores, core)
    mon = [sum(1 << e for e in rest[:n]) for n in HOME]
    others = [r for r in range(N) if r != rank]
    near = [r for r in others if topo.chip(cores[r]) == topo.chip(core)]
    far_of = lambda s: sorted((r for r in range(N) if topo.chip(cores[r]) != topo.chip(cores[s])), key=lambda r: (r - s) % N)
    far = far_of(rank)
    second_call = lambda src, dst: dst in far_of(src)[CUT["first"]:]
    incs = lambda r, step: HOME[step] if r in near and step < 2 else _masks(topo, cores, cores[r])[1]
    is_late = lambda src, dst: _blocks(topo, cores, perm, src).index(perm.index(dst)) >= CUT["late"]
    late = [r for r in others if is_late(r, rank)]
    early = [r for r in others if r not in late]

    V, A, PE, S = g.vector, g.scalar, g.tensor, g.sync
    ops = []

    def op(e, f, r=(), w=(), b=(), tok=None, dma=False):
        ops.append({"e": e, "f": f, "r": list(r), "w": list(w), "b": list(b), "tok": tok, "dma": dma,
                    "used": False, "n": len(ops)})

    def ts(out, in0, s1, s2, o0, o1=None):
        if o1 is None:
            return lambda: V.tensor_scalar(out, in0, s1, None, o0)
        return lambda: V.tensor_scalar(out, in0, s1, s2, o0, o1)

    def tt(out, a, b, o):
        return lambda: V.tensor_tensor(out, a, b, o)

    def act(out, in_, func, bias=0.0, scale=1.0):
        return lambda: A.activation(out, in_, func, bias=bias, scale=scale)

    def mms(lst):
        def f():
            ins = None
            for (out, lhsT, rhs, st, sp) in lst:
                ins = PE.matmul(out, lhsT, rhs, st, sp)
            return ins
        return f

    def iota(out, pattern, base, cm, flt):
        if flt:
            return lambda: g.iota(out, pattern, base, cm, allow_small_or_imprecise_dtypes=True)
        return lambda: g.iota(out, pattern, base, cm)

    CX, CZ, KB, KR = 0, 72, 72, 99
    sell, seld, sele = T.sel[:, 0:16], T.sel[:, 16:32], T.sel[:, 32:48]
    zeros = T.winc[:, 0:128]

    def mark(out, name, pattern, base, cm, value=1.0, src=None, test=ALU.not_equal, after=("wcy",)):
        n = 1
        for _step, count in pattern:
            n *= count
        src = T.winc[0:out.shape[0], 0:n] if src is None else src
        op("pool", lambda: g.affine_select(out, src, pattern, test, value, base, cm), r=after, w=[name])

    def cam_load(q, after):
        op("sync", lambda: S.dma_start(T.winc[16 * q:16 * q + 16, 128:4224], T.cam[:]), r=after, w=["winc%d" % q], tok=("dc", 128), dma=True)

    ctall = ["ct%d" % k for k in range(9)]
    op("sync", lambda: S.dma_start(T.lensi[:], T.lens[:]), w=["lensi"], tok=("dl", 16), dma=True)
    op("act", lambda: A.dma_start(T.posei[0:8, 0:6], T.pose[:]), w=["posei"], tok=("dp", 16), dma=True)
    op("dve", lambda: V.memset(zeros, 0.0), w=["wcy"])
    op("dve", lambda: V.memset(T.winl[:, 0:CUT["fill"][0]], 0.0), w=["wl0"])
    for q in range(CUT["early"]):
        cam_load(q, ["wl0"])
    fill, end = ["wl0", "wl1"], WL
    for k, n in enumerate(CUT["fill"][1:]):
        op("act", act(T.winl[:, end - n:end], T.winl[:, 0:n], AF.Copy), r=["wl0"], w=["wl%d" % (k + 2)])
        fill, end = fill + ["wl%d" % (k + 2)], end - n
    op("dve", lambda: V.memset(T.winl[:, CUT["fill"][0]:end], 0.0), w=["wl1"])

    def table(r, src, name):
        op("sync", lambda: S.dma_start(T.winl[r:128:16, 16:4112], src[:, :]), r=[name] + fill, w=["wl" + name], tok=("dw", 48), dma=True)

    op("dve", lambda: V.memset(T.ct[:, :], 0.0), w=["ct"] + ctall)
    op("dve", lambda: V.memset(T.ct[:, CZ + 70:CZ + KR:28], -7.0 / 16), w=["ct0"])
    op("pool", iota(T.d16[:, :], [[-1, 16]], 0, 1, False), w=["d16"])
    mark(T.rep[0:8, :], "rep", [[1, 8], [0, 16]], 0, -1)
    mark(T.idbf[:, :], "idbf", [[-1, 128]], 0, 1)
    for h in range(2):
        op("pool", iota(T.kk[0:64, 128 * h:128 * h + 128], [[16, 4], [1, 8], [0, 4]], 8 * h, 0, True), w=["kk%d" % (2 * h), "kk%d" % (2 * h + 1)])
    op("pool", iota(T.kx[:, :], [[0, 64], [16, 4]], 0, 0, True), w=["kx"])
    by_height = [[-16, 8]]
    mark(T.pm[:, :], "pm", [[-1, 16], [-16, 8]], 0, 1)
    mark(sell, "sell0", [[-2, 2], [-16, 8]], 0, 1, 2.0 ** -12)
    mark(T.sel[:, 17:32:2], "seld1", by_height, 0, 1)
    op("pool", iota(T.wsc[:, 8:10], [[-128, 2]], 64, 0, True), w=["w64"])
    op("pool", iota(T.wsc[:, 10:12], [[-62, 2]], 31, 0, True), w=["w31"])
    mark(T.sel[:, 0:8], "sell1", by_height, -1, 1, 2.0 ** -12, T.sel[:, 0:8], after=["sell0", "seld1", "w64", "w31"])
    mark(T.sel[:, 17:32:2], "seld2", by_height, -1, 1, 2.0 ** -9, T.sel[:, 17:32:2], after=["seld1"])
    mark(T.sel[:, 16:32:2], "seld0", by_height, -15, 1, 16.0)
    op("pool", iota(T.winc[:, 4224:WC], [[0, WC - 4224]], 0, 0, True), w=["wcz"])
    mark(T.rst[:, :], "rst", [[0, 16], [1, 8]], 0, 0, test=ALU.is_equal)
    mark(T.sel[:, 32:40], "sele0", by_height, -15, 1, -16.0)
    mark(T.sel[:, 40:48], "sele1", by_height, -15, 1, 16.0)
    for k, (c0, value, base, cm) in enumerate(((9, -0.125, -16, 1), (8, -0.125, -16, 1), (9, 0.125, -16, 1),
                                               (10, 31.0 / 512, 15, -1), (11, -31.0 / 512, 15, -1))):
        mark(T.wsc[:, k:k + 1], "wsc%d" % k, [[0, 1]], base, cm, value, T.wsc[:, c0:c0 + 1], ALU.is_ge, ["w64", "w31"])
    op("dve", lambda: V.tensor_copy(T.poseb[0:8, 0:6], T.posei[0:8, 0:6]), r=["posei"], w=["poseh"])
    op("dve", ts(T.ii[:, 0:1], T.d16[:, 0:1], 3, None, ALU.bitwise_and), r=["d16"], w=["ii0"])
    op("dve", tt(T.poseb[0:8, 6:12], T.posei[0:8, 0:6], T.poseb[0:8, 0:6], ALU.subtract), r=["posei", "poseh"], w=["posel"])
    op("dve", ts(T.ii[:, 1:2], T.d16[:, 0:1], 12, None, ALU.bitwise_and), r=["d16"], w=["ii1"])
    op("pe", mms([(T.p6[:, 0:12], T.rep[0:8, :], T.poseb[0:8, 0:12], True, True)]), r=["rep", "poseh", "posel"], b=["p6"])
    op("pe", mms([(T.pc1[:, 0:2], T.rep[0:8, :], T.poseb[0:8, 4:6], True, False), (T.pc1[:, 0:2], T.rep[0:8, :], T.poseb[0:8, 10:12], False, True)]),
       r=["rep", "poseh", "posel"], b=["pc1"])
    op("dve", lambda: V.tensor_copy(T.hi[:, :], T.lensi[:, :]), r=["lensi"], w=["hi"])
    op("dve", ts(T.col[:, 0:2], T.ii[:, :], -1.0, None, ALU.mult), r=["ii0", "ii1"], w=["icol"])
    for k, (out, src, scale) in enumerate((
            (T.ct[:, CX:CZ + 1:CZ], T.p6[:, 0:2], -1.0), (T.ct[:, CZ + 32:CZ + 33], T.p6[:, 0:1], 1.0),
            (T.ct[:, CZ + 64:CZ + 66], T.p6[:, 3:10:6], 0.125), (T.ct[:, CX + 66:CZ + 67:CZ], T.p6[:, 0:2], T.col[:, 0:1]),
            (T.ct[:, CX + 67:CZ + 68:CZ], T.p6[:, 0:2], T.col[:, 1:2]), (T.ct[:, CZ + 96:CZ + 98], T.p6[:, 5:12:6], -1.0),
            (T.ct[:, CX + 32:CX + 33], T.p6[:, 1:2], -1.0), (T.ct[:, CX + 64:CX + 66], T.p6[:, 2:9:6], -0.125))):
        op("act", act(out, src, AF.Identity, scale=scale), r=["icol"], w=[ctall[k + 1]], b=["p6"])
    table(0, T.hi, "hi")
    op("pe", mms([(T.pb1[:, 0:256], T.idbf[:, :], T.hi[:, :], True, True)]), r=["idbf", "hi"], b=["pb1"])
    op("dve", ts(T.vt[:, :], T.lensi[:, :], T.pc1[:, 0:1], 4096 * 207.5 + 0.5, ALU.mult, ALU.add), r=["lensi"], w=["vt"], b=["pc1"])
    table(2, T.vt, "vt")
    op("dve", tt(T.lo[:, :], T.lensi[:, :], T.pb1[:, 0:256], ALU.subtract), r=["lensi"], w=["lo"], b=["pb1"])
    table(1, T.lo, "lo")
    op("dve", lambda: V.memset(T.kk[64:128, :], 1.0), w=["kk64"])
    op("dve", lambda: V.tensor_copy(T.kk[0:32, :], T.kx[:, :]), r=["kx"], w=["kk0", "kk2"])
    op("pe", mms([(T.p7[0:KR, 128:256], T.ct[:, CZ:CZ + KR], T.idbf[:, :], True, True)]), r=["ct", "idbf"] + ctall[:7], b=["p7"])
    op("pe", mms([(T.pc0[0:KB, 0:128], T.ct[:, CX:CX + KB], T.idbf[:, :], True, True)]), r=["ct", "idbf"] + ctall, b=["pc0"])
    op("act", act(T.pt[0:KR, 128:256], T.p7[0:KR, 128:256], AF.Copy), w=["ptz"], b=["p7"])
    op("act", act(T.pt[0:KB, 0:128], T.pc0[0:KB, 0:128], AF.Copy), w=["ptx"], b=["pc0"])
    kkall = ["kk0", "kk1", "kk2", "kk3", "kk64"]
    kkof = lambda h: kkall[2 * h:2 * h + 2] + ["kk64"]
    half = lambda t, h, r0=0, r1=KB: t[r0:r1, 128 * h:128 * h + 128]

    def z_base(h, stop):
        op("pe", mms([(T["pa%d" % h][:, 0:128], T.pt[0:KB, 128:256], half(T.kk, h), True, stop)]), r=kkof(h) + ["ptz"], b=["pa%d" % h])

    def x_base(h, stop):
        op("pe", mms([(T["pb%d" % h][:, 256:384], half(T.kk, h), T.pt[0:KB, 0:128], True, stop)]), r=kkof(h) + ["ptx"], b=["pb%d" % h])

    def d_base(h):
        pc = T["pc%d" % h]
        op("pe", mms([(pc[:, 0:256:2], half(T.kk, h), T.pt[0:KB, 256:384], True, False),
                      (pc[:, 1:256:2], half(T.kk, h, 0, 32), T.winc[0:32, 0:128], False, False)]), r=kkall + ["ptd", "wcy"], b=["pc%d" % h])

    def a_zo(p, h):
        n = "%d%d" % (p, h)
        op("dve", ts(T["zo" + n][:, :], T["pa%d" % h][:, 0:128], 16.0, 4112.0, ALU.add, ALU.min), w=["zo" + n], b=["pa%d" % h])

    def a_x(p, h):
        n = "%d%d" % (p, h)
        op("dve", ts(T["xi" + n][:, :], T["pb%d" % h][:, 256:384], -0.25, -15.5 / 32, ALU.mult, ALU.add), w=["xi" + n], b=["pb%d" % h])

    wl = fill + ["wlhi", "wllo", "wlvt"]
    wc = ["winc%d" % q for q in range(8)] + ["wcz", "wcy"]
    gall = lambda out, k0=0, k1=128: ["%s_%d" % (out, k) for k in range(k0, k1, 2)]

    def tile(name, k0=0, k1=128):
        if name[:3] in ("zo1", "xi1"):
            return T[name[:3]][:, 128 * int(name[3]) + k0:128 * int(name[3]) + k1]
        return T[name][:, k0:k1]

    def gather(e, out, off, k0, k1):
        lens = out[:2] == "gl"
        win = T.winl[:, 0:WL] if lens else T.winc[:, 0:WC]
        src = lambda: win.indirect(tile(off, k0, k1))
        dst = T[out][:, 16 * k0:16 * k1]
        if e == "dve":
            f = lambda: V.tensor_copy(dst, src())
        else:
            f = lambda: A.activation(dst, src(), AF.Copy)
        op(e, f, r=[off] + (wl if lens else wc), w=gall(out, k0, k1))

    span = {}

    def piece(e, out, n=None):
        key = out
        if out[0] == "b":
            h, t = divmod(seq[int(out[1])], 4)
            out, off, ends = "gf%d" % h, "fo%d" % h, [32 * t, 32 * t + 32]
        else:
            off, ends = {"gl": "zo", "gd": "po"}[out[:2]] + out[2:], [0, 128]
        lo, hi = span.setdefault(key, ends)
        n = hi - lo if n is None else n
        assert 0 <= n <= hi - lo
        if n and e == "v":
            gather("dve", out, off, lo, lo + n)
            span[key][0] += n
        elif n:
            gather("act", out, off, hi - n, hi)
            span[key][1] -= n

    def x_lens(p, h, k0=0, k1=128):
        n = "%d%d" % (p, h)
        pb, gl = T["pb%d" % h], T["gl" + n]
        op("pe", mms([(pb[k0:k1, i:256:16], gl[:, 16 * k0 + i:16 * k1:16], sell, True, True) for i in range(16)]),
           r=gall("gl" + n, k0, k1) + ["sell0", "sell1"], b=["pb%d" % h])

    def b_w(p, h):
        n = "%d%d" % (p, h)
        op("dve", tt(T["w" + n][:, :], tile("xi" + n), T["pb%d" % h][:, 0:128], ALU.mult), r=["xi" + n], w=["w" + n], b=["pb%d" % h])

    def b_v(p, h):
        n = "%d%d" % (p, h)
        op("act", act(T["vb" + n][:, :], T["pb%d" % h][:, 128:256], AF.Identity, scale=128.0), w=["vb" + n], b=["pb%d" % h])

    def b_q(p, h):
        n = "%d%d" % (p, h)
        op("act", act(T["q" + n][:, :], T["w" + n][:, :], AF.Abs, bias=0.5, scale=4096.0), r=["w" + n], w=["q" + n])

    def pixel(p, h, c0, stop):
        n = "%d%d" % (p, h)
        out = T["pa%d" % h][:, c0:c0 + 128]
        op("pe", mms([(out, T["ub" + n][:, :], T.idbf[:, :], True, False), (out, T["vb" + n][:, :], T.idbf[:, :], False, stop)]),
           r=["vb" + n, "ub" + n, "idbf"], b=["pa%d" % h])

    def b_u(p, h):
        n = "%d%d" % (p, h)
        op("dve", ts(T["ub" + n][:, :], T["w" + n][:, :], 191.5 + 2.0 ** -13, 128.0, ALU.add, ALU.max), r=["w" + n], w=["ub" + n])

    def b_off(p, h):
        n = "%d%d" % (p, h)
        op("dve", ts(T["po" + n][:, :], T["pa%d" % h][:, 128:256], POFF, 4224.0, ALU.subtract, ALU.min), w=["po" + n], b=["pa%d" % h])

    def b_pen(p, h):
        n = "%d%d" % (p, h)
        pc, pen = T["pc%d" % h], T["pen" + n]
        op("act", act(pen[:, :], T["q" + n][:, :], AF.Relu, bias=-(2.0 ** 35), scale=2.0 ** 17), r=["q" + n], w=["pen" + n])
        if p == 1:
            op("pe", mms([(pc[:, 2 * x:256:16], T.idbf[:, :], pen[:, 16 * x:16 * x + 16], False, False) for x in range(8)]),
               r=["pen" + n, "idbf"], b=["pc%d" % h])
        else:
            op("pe", mms([(pc[:, 0:128], T.idbf[:, :], pen[:, :], False, False)]), r=["pen" + n, "idbf"], b=["pc%d" % h])
            pixel(p, h, 256, False)

    def x_depth(p, h, k0=0, k1=128):
        n = "%d%d" % (p, h)
        pc, gd = T["pc%d" % h], T["gd" + n]
        last = k0 <= 32 < k1
        lst = [(pc[k0:k1, 16 * i:16 * i + 16] if p == 1 else pc[k0:k1, i:256:16], gd[:, 16 * k0 + i:16 * k1:16],
                seld if p == 1 else sele, False, last and i == 15) for i in range(16)]
        op("pe", mms(lst), r=gall("gd" + n, k0, k1) + (["seld0", "seld2"] if p == 1 else ["sele0", "sele1"]), b=["pc%d" % h])

    def c_abs(h):
        op("act", act(T["ab%d" % h][:, :], T["pc%d" % h][:, 0:256:2], AF.Abs), w=["ab%d" % h], b=["pc%d" % h])

    def c_sums(h):
        pc, sc, snd = T["pc%d" % h], T["sc%d" % h], T["snd%d" % h]
        mk, mv = T["mk%d" % h], T["mv%d" % h]
        return [
            lambda: op("dve", tt(mk[:, :], T["ab%d" % h][:, :], T.p6[:, 128:256], ALU.is_le), r=["ab%d" % h], w=["mk%d" % h], b=["p6"]),
            lambda: op("dve", tt(mv[:, :], mk[:, :], pc[:, 1:256:2], ALU.mult), r=["mk%d" % h], w=["mv%d" % h], b=["pc%d" % h]),
            lambda: op("dve", lambda: V.tensor_tensor_scan(sc[:, :], T.rst[:, :], mv[:, :], 0.0, ALU.mult, ALU.add),
                       r=["mv%d" % h, "rst"], w=["sc%d" % h]),
            lambda: op("dve", ts(snd[:, 0:16], sc[:, 7:128:8], MAGIC, MAGIC, ALU.add, ALU.subtract), r=["sc%d" % h], w=["sna%d" % h]),
            lambda: op("dve", tt(snd[:, 16:32], sc[:, 7:128:8], snd[:, 0:16], ALU.subtract), r=["sc%d" % h, "sna%d" % h], w=["snb%d" % h])]

    def ab_base(h):
        pc = T["pc%d" % h]
        op("pe", mms([(pc[:, 0:256], T["sh%d" % h][:, :], T.ww[:, 128:384], True, False),
                      (pc[:, 0:128], half(T.kk, h, 0, KR), T.pt[0:KR, 128:256], False, False),
                      (pc[:, 128:256], half(T.kn, h), T.pt[0:KB, 128:256], False, False)]),
           r=kkall + ["kn", "ptz", "ww1", "ww2", "sh%d" % h], w=["test%d" % h], b=["pc%d" % h])
        op("pe", mms([(pc[:, 128:256], half(T.kk, h, 96, KR), T.pt[96:KR, 128:256], False, False)]), r=["test%d" % h], b=["pc%d" % h])

    def c_fail(h):
        pa, gb = T["pa%d" % h], T["gb%d" % h]
        op("act", act(gb[:, :], T["pc%d" % h][:, 0:256], AF.Relu, scale=2.0 ** 24), w=["gb%d" % h], b=["pc%d" % h])
        op("pe", mms([(pa[:, 256:384], gb[:, 128 * x:128 * x + 128], T.idbf[:, :], False, x == 1) for x in range(2)]),
           r=["gb%d" % h, "idbf"], b=["pa%d" % h])

    def c_off(h):
        op("dve", ts(T["fo%d" % h][:, :], T["pa%d" % h][:, 256:384], POFF, 4224.0, ALU.subtract, ALU.min), w=["fo%d" % h], b=["pa%d" % h])

    left = [0]

    def dst_id(r):
        rid, pid, _se = topo.addr(cores[r])
        return DstId(rid=rid, pnc=pid)

    def send_shift(h):
        snd, land = T["snd%d" % h][:, :], T["rcv%d" % h][:, rank, :]

        def call(sem, *parts):
            tr = [RemoteDMATransfer(dst_ids=[dst_id(r) for r in grp], dma_engine_mask=m, remote_sem=T.sem[sem],
                                    srcs=[snd], dsts=[land for _r in grp]) for grp, m in parts]
            op("pool", lambda: g.remote_dma_fused(tr, local_sem=T.sem.ls), r=["sna%d" % h, "snb%d" % h], tok=("ls", 0))
        second = [r for r in far if second_call(rank, r)]
        call("xa%d" % h, ([r for r in far if r not in second], moff), (near, mon[h]))
        left[0] += noff + HOME[h]
        if second:
            call("xb%d" % h, (second, moff))
            left[0] += noff

    sbank = ("p7", "p6")

    def shift_own(h):
        op("pe", mms([(T[sbank[h]][0:32, 384:512], T["snd%d" % h][:, :], T.idbf[:, :], True, False)]),
           r=["sna%d" % h, "snb%d" % h, "idbf"], b=[sbank[h]])

    def shift_sum(h):
        second = [r for r in others if second_call(r, rank)]
        groups = [(s, grp) for s, grp in (("xa%d" % h, [r for r in others if r not in second]), ("xb%d" % h, second)) if grp]
        for s, grp in groups:
            op("ext", None, w=[s], tok=(s, sum(incs(r, h) for r in grp)))
            op("pe", mms([(T[sbank[h]][0:32, 384:512], T["rcv%d" % h][:, r, :], T.idbf[:, :], False, r == groups[-1][1][-1]) for r in grp]),
               r=[s], b=[sbank[h]])

    def shift_clamp(h):
        pa, pb, sh = T["pa%d" % h], T["pb%d" % h], T["sh%d" % h]
        op("dve", ts(sh[:, :], T[sbank[h]][0:32, 384:512], T.wsc[:, 4:5], T.wsc[:, 3:4], ALU.max, ALU.min),
           r=["wsc3", "wsc4"], w=["sh%d" % h], b=[sbank[h]])
        op("pe", mms([(pa[:, 0:128], T.ww[:, 128:256], sh[:, :], False, True)]), r=["ww1", "sh%d" % h], b=["pa%d" % h])
        op("pe", mms([(pb[:, 256:384], sh[:, :], T.ww[:, 0:128], False, True)]), r=["ww0", "sh%d" % h], b=["pb%d" % h])

    def shift_weights():
        for k in range(3):
            op("act", act(T.wt[:, 16 * k:16 * k + 16], T.selc[:, :], AF.Identity, scale=T.col[:, 4 + k % 2:5 + k % 2]),
               r=["selc", "abf"], w=["wt%d" % k])

    def turn_weights():
        op("pe", mms([(T.p7[0:32, 128 * k:128 * k + 128], T.wt[:, 16 * k:16 * k + 32], T.idbf[:, :], True, True) for k in range(2)]),
           r=["wt0", "wt1", "wt2", "idbf"], b=["p7"])

    def keep_weights():
        for k, c0 in ((1, 128), (0, 0), (2, 128)):
            op("act", act(T.ww[:, 128 * k:128 * k + 128], T.p7[0:32, c0:c0 + 128], AF.Identity, scale=T.wsc[:, k:k + 1]),
               r=["wsc%d" % k], w=["ww%d" % k], b=["p7"])

    fbank = lambda j: (("pb0", "pc0", "pa0")[j % 3], 64 * (j // 3))

    def f_sum(b, j):
        h, t = divmod(b, 4)
        bk, c0 = fbank(j)
        gf = T["gf%d" % h]
        op("pe", mms([(T[bk][:, c0 + x:c0 + 64:4], gf[:, 512 * t + 128 * x:512 * t + 128 * x + 128], T.selc[:, :], True, True) for x in range(4)]),
           r=gall("gf%d" % h, 32 * t, 32 * t + 32) + ["selc"], b=[bk])

    def f_out(b, j):
        bk, c0 = fbank(j)
        owner = perm[b]
        src = T.fout[:, b, :]
        op("dve", lambda: V.tensor_copy(src, T[bk][:, c0:c0 + 64]), w=["fout%d" % b], b=[bk])
        if owner != rank:
            rid, pid, _se = topo.addr(cores[owner])
            left[0] += noff
            sem = T.sem["fb" if is_late(rank, owner) else "fa"]
            op("pool", lambda: g.remote_dma(T.frecv[:, rank, :], src, sem, T.sem.ls, pid, rid, moff), r=["fout%d" % b], tok=("ls", 0))

    op("pe", mms([(T.pa0[:, 0:256], T.pt[0:KB, 128:256], T.kk[0:KB, :], True, True)]), r=kkall + ["ptz"], b=["pa0"])
    op("pe", mms([(T.pb0[:, 256 + 128 * h:384 + 128 * h], half(T.kk, h), T.pt[0:KB, 0:128], True, True) for h in range(2)]),
       r=kkall + ["ptx"], b=["pb0"])
    op("dve", ts(T.zo1[:, :], T.pa0[:, 0:256], 16.0, 4112.0, ALU.add, ALU.min), w=["zo10", "zo11"], b=["pa0"])
    for q in range(CUT["early"], 8):
        cam_load(q, [CUT["gate"]])
    op("dve", ts(T.xi1[:, :], T.pb0[:, 256:512], -0.25, -15.5 / 32, ALU.mult, ALU.add), w=["xi10", "xi11"], b=["pb0"])
    op("pe", mms([(T.p7[0:KR, 256:384], T.ct[:, CZ:CZ + KR], T.pm[:, :], True, True)]), r=["ct", "pm"] + ctall, b=["p7"])

    def more(k):
        if k == 0:
            op("dve", ts(T.d16a[:, :], T.d16[:, :], 15, None, ALU.bitwise_and), r=["d16"], w=["d16a"])
            op("dve", ts(T.selc[:, :], T.d16a[:, :], 0.0, None, ALU.is_equal), r=["d16a"], w=["selc"])
        elif k == 1:
            op("dve", lambda: V.tensor_copy(T.id16[:, :], T.idbf[:, :]), r=["idbf"], w=["id16"])
        elif k == 2:
            op("act", act(T.col[:, 4:6], T.p6[:, 0:2], AF.Copy), w=["abf"], b=["p6"])
        elif k == 3:
            op("dve", ts(T.kn[0:KB, :], T.kk[0:KB, :], -1.0, None, ALU.mult), r=kkall, w=["kn"])
        else:
            op("act", act(T.pt[0:KR, 256:384], T.p7[0:KR, 256:384], AF.Identity, scale=-1.0), w=["ptd"], b=["p7"])
            d_base(0)
            d_base(1)
            op("pe", mms([(T.p6[:, 128:256], half(T.kk, 0, 96, KR), T.pt[96:KR, 256:384], True, True)]), r=["kk64", "ptd"], b=["p6"])

    seq = _blocks(topo, cores, perm, rank)
    sums = [c_sums(0), c_sums(1)]
    by_pass = {"lens": x_lens, "w": b_w, "row": b_v, "q": b_q, "u": b_u, "turn": lambda p, h: pixel(p, h, 128, True),
               "off": b_off, "pen": b_pen, "depth": x_depth, "z": a_zo, "x": a_x}
    by_half = {"abs": c_abs, "sum": lambda h: sums[h].pop(0)(), "send": send_shift, "own": shift_own, "add": shift_sum, "clamp": shift_clamp,
               "base": lambda h: (z_base(h, False), x_base(h, False)), "test": ab_base, "fail": c_fail, "last": c_off,
               "weights": lambda k: (shift_weights, turn_weights, keep_weights)[k](), "more": more,
               "fold": lambda j: f_sum(seq[j], j), "out": lambda j: f_out(seq[j], j)}
    for step in PLAN.split():
        if step[1] == ":":
            e, out, n = (step.split(":") + [None])[:3]
            piece(e, out, n and int(n))
        elif ":" in step:
            name, k0, k1 = step.split(":")
            by_pass[name[:-2]](int(name[-2]), int(name[-1]), int(k0), int(k1))
        elif step[:-2] in by_pass:
            by_pass[step[:-2]](int(step[-2]), int(step[-1]))
        else:
            by_half[step[:-1]](int(step[-1]))
    assert all(lo == hi for lo, hi in span.values())
    op("pe", mms([(T.p6[0:64, 256:384], T.fout[:, seq[7], :], T.id16[:, :], True, False)]), r=["fout%d" % seq[7], "id16"], b=["p6"])
    groups = [(s, grp) for s, grp in (("fa", early), ("fb", late)) if grp]
    for s, grp in groups:
        op("ext", None, w=[s], tok=(s, sum(incs(r, 2) for r in grp)))
        op("pe", mms([(T.p6[0:64, 256:384], T.frecv[:, r, :], T.id16[:, :], False, s == groups[-1][0] and r == grp[-1]) for r in grp]),
           r=[s], b=["p6"])
    op("act", act(T.yb[:, :], T.p6[0:64, 256:384], AF.Copy), w=["yb"], b=["p6"])
    op("act", lambda: A.dma_start(T.y[:], T.yb[:, :]), r=["yb"], tok=("dy", 16), dma=True)
    _emit(g, T, ops)
    g.wait_ge(T.sem.ls, left[0])
    A.wait_ge(T.sem.dy, 16)
